import numpy as np
import ml_dtypes


def mxq(x, axis, fmt="e4m3"):
    dtype, down = {"e4m3": (ml_dtypes.float8_e4m3fn, 7), "e5m2": (ml_dtypes.float8_e5m2, 14)}[fmt]
    v = np.moveaxis(np.asarray(x, np.float32).astype(ml_dtypes.bfloat16).astype(np.float64), axis, -1)
    blocks = v.reshape(v.shape[:-1] + (-1, 32))
    amax = np.abs(blocks).max(-1, keepdims=True)
    byte = np.maximum(np.where(amax > 0, np.frexp(amax)[1] - 1 + 127, 0) - down, 1)
    scale = np.exp2(byte - 127.0)
    codes = (blocks / scale).astype(np.float32).astype(dtype).astype(np.float64)
    return np.moveaxis((codes * scale).reshape(v.shape), -1, axis)


WIDE = False


def mx_kscale(k):
    if not WIDE:
        return np.ones(k)
    levels = np.array([30, -30])
    if k % 512:
        return np.exp2(np.random.permutation(np.resize(levels, k // 32))).repeat(32)
    a = np.empty((k // 512, 16))
    for p in range(k // 512):
        a[p, :8] = np.random.permutation(np.resize(levels, 8))
        for g in range(8):
            far = levels[np.abs(levels - a[p, g]) >= 10]
            a[p, g + 8] = far[np.random.randint(len(far))]
    return np.exp2(a.ravel()).repeat(32)


BF16 = ml_dtypes.bfloat16


def bf(x):
    return np.asarray(x, np.float32).astype(BF16)


def f64(x):
    return np.asarray(x).astype(np.float64)


E2M1 = np.array([0.0, 0.5, 1.0, 1.5, 2.0, 3.0, 4.0, 6.0, -0.0, -0.5, -1.0, -1.5, -2.0, -3.0, -4.0, -6.0])


def pack_weight(w, fmt):
    k, n = w.shape
    w = f64(bf(w)).reshape(k // 32, 32, n)
    amax = np.abs(w).max(1)
    if fmt == "e4m3":
        byte = np.frexp(amax)[1] - 1 + 127 - 7
    else:
        mant, ex = np.frexp(amax / 6.0)
        byte = np.where(mant > 0.5, ex, ex - 1) + 127
    byte = np.clip(np.where(amax > 0, byte, 1), 1, 254)
    scaled = (w * np.exp2(127.0 - byte)[:, None, :]).reshape(k, n).astype(np.float32)
    by_word = np.ascontiguousarray(scaled.reshape(k // 512, 128, 4, n).transpose(0, 1, 3, 2))
    if fmt == "e4m3":
        words = by_word.astype(ml_dtypes.float8_e4m3fn).view(np.uint8)
    else:
        c = by_word.astype(ml_dtypes.float4_e2m1fn).view(np.uint8) & 0xF
        words = c[..., 0::2] | (c[..., 1::2] << 4)
    return np.ascontiguousarray(words), np.ascontiguousarray(byte.astype(np.uint8).reshape(k // 512, 16, n))


def unpack_weight(words, scales, fmt):
    g, p, n, _ = words.shape
    if fmt == "e4m3":
        vals = np.ascontiguousarray(words).view(ml_dtypes.float8_e4m3fn).astype(np.float64)
    else:
        nib = np.empty((g, p, n, 4), np.uint8)
        nib[..., 0::2] = words & 0xF
        nib[..., 1::2] = words >> 4
        vals = E2M1[nib]
    vals = vals * np.repeat(np.exp2(scales.astype(np.float64) - 127.0), 8, axis=1)[..., None]
    return vals.transpose(0, 1, 3, 2).reshape(g * 512, n)
def pack4(w):
    words, scales = pack_weight(w, "e2m1")
    return words.reshape(words.shape[0], 128, -1), scales


def unpack4(words, scales):
    return unpack_weight(words.reshape(words.shape[0], 128, -1, 2), scales, "e2m1")


T, D, S, V = 512, 1024, 1024, 2048


def setup_inputs():
    s = mx_kscale(D)
    t = mx_kscale(S)
    x = np.random.standard_normal((T, D)) * s
    wd = 0.7 * np.random.standard_normal((D, S)) / np.sqrt(D) / s[:, None]
    wd_words, wd_scales = pack4(wd)
    wf = np.random.standard_normal((D, V)) / np.sqrt(D) / s[:, None]
    prior = (1 + 0.1 * np.random.standard_normal(S)) * t
    c = np.random.standard_normal((S, V)) / np.sqrt(S) / t[:, None]
    bias = 0.3 * np.random.standard_normal(V)
    return {"x": bf(x), "wd_words": wd_words, "wd_scales": wd_scales,
            "wf": bf(wf), "prior": bf(prior), "c": bf(c), "bias": bf(bias)}


def reference(x, wd_words, wd_scales, wf, prior, c, bias):
    xq = mxq(f64(x), 1, "e4m3")
    draft = xq @ unpack4(wd_words, wd_scales)
    e = np.exp(draft) * f64(prior)
    head = xq @ mxq(f64(wf), 0, "e4m3")
    corr = mxq(e, 1, "e5m2") @ mxq(f64(c), 0, "e4m3")
    full = head + corr + f64(bias)
    return draft, full

@@ -1,0 +1,296 @@
+from contextlib import ExitStack
+
+import concourse.mybir as mybir
+from concourse.masks import make_identity
+
+T, D, S, V = 512, 1024, 1024, 2048
+FLOPS = 2 * T * D * S + 2 * T * D * V + 2 * T * S * V
+
+F32 = mybir.dt.float32
+BF16 = mybir.dt.bfloat16
+I32 = mybir.dt.int32
+U32 = mybir.dt.uint32
+U8 = mybir.dt.uint8
+E4M3 = mybir.dt.float8_e4m3fn_x4
+E5M2 = mybir.dt.float8_e5m2_x4
+E2M1 = mybir.dt.float4_e2m1fn_x4
+ACT = mybir.ActivationFunctionType
+ALU = mybir.AluOpType
+
+P = 128
+W = 512
+
+
+def tile_draft_logit_correction_s9_kernel(tc, x, wd_words, wd_scales, wf, prior, c, bias, draft, full):
+    nc = tc.nc
+    with ExitStack() as ctx:
+        keep = ctx.enter_context(tc.tile_pool(name="keep", bufs=1))
+        work = ctx.enter_context(tc.tile_pool(name="work", bufs=2))
+        psum = ctx.enter_context(tc.psum_pool(name="psum", bufs=8))
+        ctx.enter_context(tc.manual_schedule())
+
+        warm = keep.tile([P, 1], F32)
+        nc.gpsimd.memset(warm[:], 0.0)
+        nc.scalar.activation(out=warm[:], in_=warm[:], func=ACT.Exp)
+        ident = keep.tile([P, P], F32)
+        make_identity(nc, ident[:])
+        ident_b = keep.tile([P, P], BF16)
+        nc.vector.tensor_copy(out=ident_b[:], in_=ident[:])
+        wd_s = keep.tile([P, 2, S], U8, align_bytes=64)
+        nc.vector.memset(wd_s[:].bitcast(I32), 0)
+
+        bias_col = keep.tile([P, 16], BF16)
+        nc.scalar.dma_start(out=bias_col[:], in_=bias.rearrange("(p i) -> p i", i=16))
+        prior_sb = keep.tile([P, 2, 4], BF16)
+        nc.scalar.dma_start(out=prior_sb[:], in_=prior.rearrange("(g p j) -> p g j", g=2, j=4))
+
+        x_sb = []
+        for i in range(4):
+            x_tile = keep.tile([P, D], BF16, name=f"x_sb{i}")
+            x_sb.append(x_tile)
+        wd_w = keep.tile([P, 2, 2 * S], U8, align_bytes=64)
+        raw = {}
+        for m in ("f0", "f1", "c0", "c1"):
+            for h in range(2):
+                raw_tile = keep.tile([P, 4, 2 * W], BF16, name=f"raw_{m}_{h}")
+                raw[m, h] = raw_tile
+
+        def load_x(i):
+            nc.sync.dma_start(out=x_sb[i][:], in_=x[P * i : P * (i + 1), :])
+
+        def src_rows(m):
+            src = wf if m[0] == "f" else c
+            g = int(m[1])
+            return src[512 * g : 512 * (g + 1), :].rearrange("(p j) n -> p j n", j=4)
+
+        def load_quarter(m, q):
+            nc.sync.dma_start(
+                out=raw[m, q // 2][:, :, W * (q % 2) : W * (q % 2 + 1)], in_=src_rows(m)[:, :, W * q : W * (q + 1)]
+            )
+
+        def load_half(m, h):
+            nc.sync.dma_start(out=raw[m, h][:], in_=src_rows(m)[:, :, 2 * W * h : 2 * W * (h + 1)])
+
+        load_x(0)
+        load_x(1)
+        load_quarter("f0", 0)
+        load_x(2)
+        load_x(3)
+        load_quarter("f1", 0)
+        scales32 = wd_scales.bitcast(I32)
+        for quad in range(4):
+            nc.sync.dma_start(
+                out=wd_s[32 * quad : 32 * quad + 4, :, :].bitcast(I32),
+                in_=scales32[:, 4 * quad : 4 * quad + 4, :].rearrange("g r n -> r g n"),
+            )
+        nc.sync.dma_start(out=wd_w[:].bitcast(I32), in_=wd_words.bitcast(I32).rearrange("g p n -> p g n"))
+        load_quarter("f0", 1)
+        load_quarter("f1", 1)
+        for h in range(2):
+            for m in ("f0", "f1", "c0", "c1"):
+                if h == 0 and m[0] == "f":
+                    continue
+                load_half(m, h)
+
+        x_g = keep.tile([P, 2, T, 4], BF16, align_bytes=64)
+        x_q = keep.tile([P, 2, T], U32, align_bytes=64)
+        x_s = keep.tile([P, 2, T], U8, align_bytes=64)
+        e_g = keep.tile([P, 2, T, 4], BF16, align_bytes=64)
+        e_q = keep.tile([P, 2, T], U32, align_bytes=64)
+        e_s = keep.tile([P, 2, T], U8, align_bytes=64)
+        bias_bc = keep.tile([P, V], BF16)
+        draft_sb = []
+        for i in range(4):
+            draft_tile = keep.tile([P, S], F32, name=f"draft_sb{i}")
+            draft_sb.append(draft_tile)
+
+        for h in range(2):
+            bank = psum.tile([P, 8, P], BF16, name="bank")
+            for i in range(8):
+                nc.tensor.transpose(
+                    bank[:, i, :], bias_col[:, 8 * h + i : 8 * h + i + 1].to_broadcast([P, P]), ident_b[:]
+                )
+            nc.scalar.copy(
+                out=bias_bc[:].rearrange("q (p i) -> q p i", i=16)[:, :, 8 * h : 8 * h + 8],
+                in_=bank[:].rearrange("q i p -> q p i"),
+            )
+
+        x_banks = {}
+
+        def turn_x(i):
+            bank = psum.tile([P, 4, P], F32, name="bank")
+            words = x_sb[i][:].bitcast(F32)
+            for g in range(2):
+                for u in range(2):
+                    nc.tensor.transpose(bank[:, 2 * g + u, :], words[:, 256 * g + u : 256 * (g + 1) : 2], ident[:])
+            x_banks[i] = bank
+
+        def copy_x(copy, i):
+            words = x_g[:].rearrange("p g t k -> p (g t k)").bitcast(F32).rearrange("p (g t u) -> p g t u", g=2, u=2)
+            copy(
+                out=words[:, :, P * i : P * (i + 1), :],
+                in_=x_banks[i][:].rearrange("p (g u) r -> p g r u", g=2),
+            )
+
+        def quant_x(g):
+            nc.vector.quantize_mx(
+                out=x_q[:, g, :].bitcast(E4M3), scales=x_s[:, g, :], in_=x_g[:, g].rearrange("p t k -> p (t k)")
+            )
+
+        grouped, codes, planes = {}, {}, {}
+
+        def lay(m, q, cut):
+            tile = work.tile([P, W, 4], BF16, name="grouped", align_bytes=64, bufs=4)
+            src = raw[m, q // 2][:, :, W * (q % 2) : W * (q % 2 + 1)]
+            for copy, lo, hi in ((nc.scalar.copy, 0, cut), (nc.vector.tensor_copy, cut, W)):
+                copy(
+                    out=tile[:, lo:hi, :].rearrange("p (c i) j -> p c j i", i=4),
+                    in_=src[:, :, lo:hi].rearrange("p j (c i) -> p c j i", i=4),
+                )
+            grouped[m, q] = tile
+
+        def quant(m, q):
+            code = keep.tile([P, W], U32, name=f"code_{m}_{q}", align_bytes=64)
+            plane = keep.tile([P, W], U8, name=f"plane_{m}_{q}", align_bytes=64)
+            nc.vector.quantize_mx(
+                out=code[:].bitcast(E4M3), scales=plane[:], in_=grouped[m, q][:].rearrange("p n j -> p (n j)")
+            )
+            codes[m, q], planes[m, q] = code, plane
+
+        d_banks, e_rows, et_banks = {}, {}, {}
+
+        def draft_mm(n):
+            g, t = divmod(n, 4)
+            bank = psum.tile([P, W], F32, name="bank")
+            for k in range(2):
+                nc.tensor.matmul_mx(
+                    out=bank[:],
+                    lhsT=x_q[:, k, P * t : P * (t + 1)].bitcast(E4M3),
+                    lhsT_scale=x_s[:, k, P * t : P * (t + 1)],
+                    rhs=wd_w[:, k, 2 * W * g : 2 * W * (g + 1)].bitcast(E2M1),
+                    rhs_scale=wd_s[:, k, W * g : W * (g + 1)],
+                    start=(k == 0),
+                    stop=(k == 1),
+                )
+            d_banks[n] = bank
+
+        def exp(n):
+            rows = work.tile([P, 4, P], F32, name="e_rows", bufs=4)
+            nc.scalar.activation(
+                out=rows[:], in_=d_banks[n][:].rearrange("t (p j) -> t j p", j=4), func=ACT.Exp
+            )
+            e_rows[n] = rows
+
+        def draft_out(copy, n):
+            g, t = divmod(n, 4)
+            copy(out=draft_sb[t][:, W * g : W * (g + 1)], in_=d_banks[n][:])
+            if g == 1:
+                nc.sync.dma_start(out=draft[P * t : P * (t + 1), :], in_=draft_sb[t][:])
+
+        def turn_e(n):
+            bank = psum.tile([P, 4, P], F32, name="bank")
+            for j in range(4):
+                nc.tensor.transpose(bank[:, j, :], e_rows[n][:, j, :], ident[:])
+            et_banks[n] = bank
+
+        def weigh_e(n):
+            g, t = divmod(n, 4)
+            nc.vector.tensor_tensor(
+                out=e_g[:, g, P * t : P * (t + 1), :],
+                in0=et_banks[n][:].rearrange("p j t -> p t j"),
+                in1=prior_sb[:, g, :].unsqueeze(1).to_broadcast([P, P, 4]),
+                op=ALU.mult,
+            )
+
+        def quant_e(g):
+            nc.vector.quantize_mx(
+                out=e_q[:, g, :].bitcast(E5M2), scales=e_s[:, g, :], in_=e_g[:, g].rearrange("p t k -> p (t k)")
+            )
+
+        acc = {}
+
+        def full_mm(m, q):
+            for t in range(4):
+                if m == "f0":
+                    bank = psum.tile([P, W], F32, name="bank")
+                    acc[q, t] = bank
+                k = int(m[1])
+                cols = slice(P * t, P * (t + 1))
+                if m[0] == "f":
+                    lhs, lhs_s = x_q[:, k, cols].bitcast(E4M3), x_s[:, k, cols]
+                else:
+                    lhs, lhs_s = e_q[:, k, cols].bitcast(E5M2), e_s[:, k, cols]
+                nc.tensor.matmul_mx(
+                    out=acc[q, t][:],
+                    lhsT=lhs,
+                    lhsT_scale=lhs_s,
+                    rhs=codes[m, q][:].bitcast(E4M3),
+                    rhs_scale=planes[m, q][:],
+                    start=(m == "f0"),
+                    stop=(m == "c1"),
+                )
+
+        def full_out(q, t):
+            tile = work.tile([P, W], F32, name="full_sb", bufs=6)
+            nc.vector.tensor_tensor(out=tile[:], in0=acc[q, t][:], in1=bias_bc[:, W * q : W * (q + 1)], op=ALU.add)
+            nc.sync.dma_start(out=full[P * t : P * (t + 1), W * q : W * (q + 1)], in_=tile[:])
+
+        vcopy, scopy = nc.vector.tensor_copy, nc.scalar.copy
+        head_cut, mid_cut, tail_cut = 256, 128, 352
+
+        for i in range(4):
+            turn_x(i)
+        copy_x(vcopy, 0)
+        copy_x(scopy, 1)
+        lay("f0", 0, head_cut)
+        copy_x(vcopy, 2)
+        copy_x(scopy, 3)
+        quant("f0", 0)
+        quant_x(0)
+        quant_x(1)
+        lay("f1", 0, head_cut)
+        full_mm("f0", 0)
+        draft_mm(0)
+        draft_mm(1)
+        quant("f1", 0)
+        mid = [("f0", 1), ("f1", 1), ("c0", 0), ("c1", 0)]
+        for n in range(8):
+            exp(n)
+            if n + 2 < 8:
+                draft_mm(n + 2)
+            turn_e(n)
+            if n % 2 == 0:
+                lay(*mid[n // 2], mid_cut)
+            elif n > 1:
+                quant(*mid[n // 2 - 1])
+            if n > 0:
+                weigh_e(n - 1)
+            draft_out(scopy, n)
+            if n == 1:
+                full_mm("f1", 0)
+            if n == 5:
+                quant_e(0)
+        weigh_e(7)
+        tail = [("c0", 1), ("c1", 1)] + [(m, q) for q in (2, 3) for m in ("f0", "f1", "c0", "c1")]
+        lay(*tail[0], tail_cut)
+        quant("c1", 0)
+        quant_e(1)
+        full_mm("c0", 0)
+        full_mm("c1", 0)
+        pending = [(0, t) for t in range(4)]
+        outs = [1, 1, 1, 1, 2, 1, 1, 1, 1, 2]
+        for k, unit in enumerate(tail):
+            if k + 1 < len(tail):
+                lay(*tail[k + 1], tail_cut)
+            quant(*unit)
+            for item in pending[: outs[k]]:
+                full_out(*item)
+            pending = pending[outs[k] :]
+            if k == 0:
+                full_mm("f0", 1)
+                full_mm("f1", 1)
+            full_mm(*unit)
+            if unit[0] == "c1":
+                pending += [(unit[1], t) for t in range(4)]
+        for item in pending:
+            full_out(*item)

@@ -19,6 +19,10 @@ ALU = mybir.AluOpType
 
 P = 128
 W = 512
+TILES = T // P
+CHUNKS = V // W
+PANELS = ("f0", "f1", "c0", "c1")
+SCALAR_COLS = 336
 
 
 def tile_draft_logit_correction_s9_kernel(tc, x, wd_words, wd_scales, wf, prior, c, bias, draft, full):
@@ -28,145 +32,121 @@ def tile_draft_logit_correction_s9_kernel(tc, x, wd_words, wd_scales, wf, prior,
         work = ctx.enter_context(tc.tile_pool(name="work", bufs=2))
         psum = ctx.enter_context(tc.psum_pool(name="psum", bufs=8))
         ctx.enter_context(tc.manual_schedule())
+        vcopy, scopy = nc.vector.tensor_copy, nc.scalar.copy
 
-        warm = keep.tile([P, 1], F32)
-        nc.gpsimd.memset(warm[:], 0.0)
-        nc.scalar.activation(out=warm[:], in_=warm[:], func=ACT.Exp)
-        ident = keep.tile([P, P], F32)
-        make_identity(nc, ident[:])
-        ident_b = keep.tile([P, P], BF16)
-        nc.vector.tensor_copy(out=ident_b[:], in_=ident[:])
-        wd_s = keep.tile([P, 2, S], U8, align_bytes=64)
-        nc.vector.memset(wd_s[:].bitcast(I32), 0)
+        x_rows = x.rearrange("(p i) d -> p i d", i=TILES)
+        draft_rows = draft.rearrange("(p i) s -> p i s", i=TILES)
+        full_rows = full.rearrange("(p i) v -> p i v", i=TILES)
 
         bias_col = keep.tile([P, 16], BF16)
         nc.scalar.dma_start(out=bias_col[:], in_=bias.rearrange("(p i) -> p i", i=16))
         prior_sb = keep.tile([P, 2, 4], BF16)
         nc.scalar.dma_start(out=prior_sb[:], in_=prior.rearrange("(g p j) -> p g j", g=2, j=4))
+        wd_s = keep.tile([P, 2, S], U8, align_bytes=64)
+        nc.vector.memset(wd_s[:].bitcast(I32), 0)
+        ident = keep.tile([P, P], F32)
+        make_identity(nc, ident[:])
 
-        x_sb = []
-        for i in range(4):
-            x_tile = keep.tile([P, D], BF16, name=f"x_sb{i}")
-            x_sb.append(x_tile)
+        x_sb, raw = {}, {}
+
+        def load_x(first, count):
+            tile = keep.tile([P, count * D], BF16, name=f"x_sb{first}")
+            nc.sync.dma_start(out=tile[:], in_=x_rows[:, first : first + count, :].rearrange("p i d -> p (i d)"))
+            for i in range(count):
+                x_sb[first + i] = tile[:, D * i : D * (i + 1)]
+
+        def load_w(panel, first, count):
+            src = wf if panel[0] == "f" else c
+            g = int(panel[1])
+            rows = src[512 * g : 512 * (g + 1), :].rearrange("(p j) n -> p j n", j=4)
+            tile = keep.tile([P, 4, W * count], BF16, name=f"raw_{panel}_{first}")
+            nc.sync.dma_start(out=tile[:], in_=rows[:, :, W * first : W * (first + count)])
+            for i in range(count):
+                raw[panel, first + i] = tile[:, :, W * i : W * (i + 1)]
+
         wd_w = keep.tile([P, 2, 2 * S], U8, align_bytes=64)
-        raw = {}
-        for m in ("f0", "f1", "c0", "c1"):
-            for h in range(2):
-                raw_tile = keep.tile([P, 4, 2 * W], BF16, name=f"raw_{m}_{h}")
-                raw[m, h] = raw_tile
-
-        def load_x(i):
-            nc.sync.dma_start(out=x_sb[i][:], in_=x[P * i : P * (i + 1), :])
-
-        def src_rows(m):
-            src = wf if m[0] == "f" else c
-            g = int(m[1])
-            return src[512 * g : 512 * (g + 1), :].rearrange("(p j) n -> p j n", j=4)
-
-        def load_quarter(m, q):
-            nc.sync.dma_start(
-                out=raw[m, q // 2][:, :, W * (q % 2) : W * (q % 2 + 1)], in_=src_rows(m)[:, :, W * q : W * (q + 1)]
-            )
-
-        def load_half(m, h):
-            nc.sync.dma_start(out=raw[m, h][:], in_=src_rows(m)[:, :, 2 * W * h : 2 * W * (h + 1)])
-
-        load_x(0)
-        load_x(1)
-        load_quarter("f0", 0)
-        load_x(2)
-        load_x(3)
-        load_quarter("f1", 0)
+        load_x(0, 1)
+        load_x(1, 1)
+        nc.sync.dma_start(out=wd_w[:].bitcast(I32), in_=wd_words.bitcast(I32).rearrange("g p n -> p g n"))
         scales32 = wd_scales.bitcast(I32)
         for quad in range(4):
             nc.sync.dma_start(
                 out=wd_s[32 * quad : 32 * quad + 4, :, :].bitcast(I32),
                 in_=scales32[:, 4 * quad : 4 * quad + 4, :].rearrange("g r n -> r g n"),
             )
-        nc.sync.dma_start(out=wd_w[:].bitcast(I32), in_=wd_words.bitcast(I32).rearrange("g p n -> p g n"))
-        load_quarter("f0", 1)
-        load_quarter("f1", 1)
-        for h in range(2):
-            for m in ("f0", "f1", "c0", "c1"):
-                if h == 0 and m[0] == "f":
-                    continue
-                load_half(m, h)
+        load_x(2, 2)
+        load_w("f0", 0, 1)
+        for panel in PANELS[1:]:
+            load_w(panel, 0, 2)
+        load_w("f0", 1, 1)
+        for panel in PANELS:
+            load_w(panel, 2, 2)
 
-        x_g = keep.tile([P, 2, T, 4], BF16, align_bytes=64)
-        x_q = keep.tile([P, 2, T], U32, align_bytes=64)
-        x_s = keep.tile([P, 2, T], U8, align_bytes=64)
-        e_g = keep.tile([P, 2, T, 4], BF16, align_bytes=64)
-        e_q = keep.tile([P, 2, T], U32, align_bytes=64)
-        e_s = keep.tile([P, 2, T], U8, align_bytes=64)
         bias_bc = keep.tile([P, V], BF16)
-        draft_sb = []
-        for i in range(4):
-            draft_tile = keep.tile([P, S], F32, name=f"draft_sb{i}")
-            draft_sb.append(draft_tile)
 
-        for h in range(2):
-            bank = psum.tile([P, 8, P], BF16, name="bank")
-            for i in range(8):
-                nc.tensor.transpose(
-                    bank[:, i, :], bias_col[:, 8 * h + i : 8 * h + i + 1].to_broadcast([P, P]), ident_b[:]
-                )
-            nc.scalar.copy(
-                out=bias_bc[:].rearrange("q (p i) -> q p i", i=16)[:, :, 8 * h : 8 * h + 8],
+        def spread_bias(h):
+            bank = psum.tile([P, 4, P], F32, name="bank")
+            words = bias_col[:].bitcast(F32)
+            for i in range(4):
+                nc.tensor.transpose(bank[:, i, :], words[:, 4 * h + i : 4 * h + i + 1].to_broadcast([P, P]), ident[:])
+            scopy(
+                out=bias_bc[:].bitcast(F32).rearrange("q (p i) -> q p i", i=8)[:, :, 4 * h : 4 * h + 4],
                 in_=bank[:].rearrange("q i p -> q p i"),
             )
 
-        x_banks = {}
+        x_banks, x_g, x_q, x_s = {}, {}, {}, {}
 
-        def turn_x(i):
+        def turn_x(t):
             bank = psum.tile([P, 4, P], F32, name="bank")
-            words = x_sb[i][:].bitcast(F32)
+            words = x_sb[t].bitcast(F32)
             for g in range(2):
                 for u in range(2):
                     nc.tensor.transpose(bank[:, 2 * g + u, :], words[:, 256 * g + u : 256 * (g + 1) : 2], ident[:])
-            x_banks[i] = bank
+            x_banks[t] = bank
 
-        def copy_x(copy, i):
-            words = x_g[:].rearrange("p g t k -> p (g t k)").bitcast(F32).rearrange("p (g t u) -> p g t u", g=2, u=2)
+        def copy_x(copy, t):
+            tile = keep.tile([P, 2 * P * 4], BF16, name=f"x_g{t}", align_bytes=64)
             copy(
-                out=words[:, :, P * i : P * (i + 1), :],
-                in_=x_banks[i][:].rearrange("p (g u) r -> p g r u", g=2),
+                out=tile[:].bitcast(F32).rearrange("p (g r u) -> p g r u", g=2, u=2),
+                in_=x_banks[t][:].rearrange("p (g u) r -> p g r u", g=2),
             )
+            x_g[t] = tile
 
-        def quant_x(g):
-            nc.vector.quantize_mx(
-                out=x_q[:, g, :].bitcast(E4M3), scales=x_s[:, g, :], in_=x_g[:, g].rearrange("p t k -> p (t k)")
-            )
+        def quant_x(t):
+            code = keep.tile([P, 2 * P], U32, name=f"x_q{t}", align_bytes=64)
+            plane = keep.tile([P, 2 * P], U8, name=f"x_s{t}", align_bytes=64)
+            nc.vector.quantize_mx(out=code[:].bitcast(E4M3), scales=plane[:], in_=x_g[t][:])
+            x_q[t], x_s[t] = code, plane
 
         grouped, codes, planes = {}, {}, {}
 
-        def lay(m, q, cut):
-            tile = work.tile([P, W, 4], BF16, name="grouped", align_bytes=64, bufs=4)
-            src = raw[m, q // 2][:, :, W * (q % 2) : W * (q % 2 + 1)]
-            for copy, lo, hi in ((nc.scalar.copy, 0, cut), (nc.vector.tensor_copy, cut, W)):
-                copy(
-                    out=tile[:, lo:hi, :].rearrange("p (c i) j -> p c j i", i=4),
-                    in_=src[:, :, lo:hi].rearrange("p j (c i) -> p c j i", i=4),
-                )
-            grouped[m, q] = tile
-
-        def quant(m, q):
-            code = keep.tile([P, W], U32, name=f"code_{m}_{q}", align_bytes=64)
-            plane = keep.tile([P, W], U8, name=f"plane_{m}_{q}", align_bytes=64)
-            nc.vector.quantize_mx(
-                out=code[:].bitcast(E4M3), scales=plane[:], in_=grouped[m, q][:].rearrange("p n j -> p (n j)")
+        def lay(copy, block, lo, hi):
+            if block not in grouped:
+                tile = work.tile([P, W, 4], BF16, name="grouped", align_bytes=64, bufs=4)
+                grouped[block] = tile
+            copy(
+                out=grouped[block][:, lo:hi, :].rearrange("p (c i) j -> p c j i", i=4),
+                in_=raw[block][:, :, lo:hi].rearrange("p j (c i) -> p c j i", i=4),
             )
-            codes[m, q], planes[m, q] = code, plane
 
-        d_banks, e_rows, et_banks = {}, {}, {}
+        def quant(block):
+            code = keep.tile([P, W], U32, name=f"code_{block[0]}_{block[1]}", align_bytes=64)
+            plane = keep.tile([P, W], U8, name=f"plane_{block[0]}_{block[1]}", align_bytes=64)
+            nc.vector.quantize_mx(
+                out=code[:].bitcast(E4M3), scales=plane[:], in_=grouped[block][:].rearrange("p n j -> p (n j)")
+            )
+            codes[block], planes[block] = code, plane
+
+        d_banks, e_rows, et_banks, e_g, e_q, e_s, draft_sb = {}, {}, {}, {}, {}, {}, {}
 
         def draft_mm(n):
-            g, t = divmod(n, 4)
+            t, g = divmod(n, 2)
             bank = psum.tile([P, W], F32, name="bank")
             for k in range(2):
                 nc.tensor.matmul_mx(
                     out=bank[:],
-                    lhsT=x_q[:, k, P * t : P * (t + 1)].bitcast(E4M3),
-                    lhsT_scale=x_s[:, k, P * t : P * (t + 1)],
+                    lhsT=x_q[t][:, P * k : P * (k + 1)].bitcast(E4M3),
+                    lhsT_scale=x_s[t][:, P * k : P * (k + 1)],
                     rhs=wd_w[:, k, 2 * W * g : 2 * W * (g + 1)].bitcast(E2M1),
                     rhs_scale=wd_s[:, k, W * g : W * (g + 1)],
                     start=(k == 0),
@@ -176,16 +156,17 @@ def tile_draft_logit_correction_s9_kernel(tc, x, wd_words, wd_scales, wf, prior,
 
         def exp(n):
             rows = work.tile([P, 4, P], F32, name="e_rows", bufs=4)
-            nc.scalar.activation(
-                out=rows[:], in_=d_banks[n][:].rearrange("t (p j) -> t j p", j=4), func=ACT.Exp
-            )
+            nc.scalar.activation(out=rows[:], in_=d_banks[n][:].rearrange("t (p j) -> t j p", j=4), func=ACT.Exp)
             e_rows[n] = rows
 
-        def draft_out(copy, n):
-            g, t = divmod(n, 4)
-            copy(out=draft_sb[t][:, W * g : W * (g + 1)], in_=d_banks[n][:])
+        def draft_out(n):
+            t, g = divmod(n, 2)
+            if g == 0:
+                tile = keep.tile([P, S], F32, name=f"draft_sb{t}")
+                draft_sb[t] = tile
+            scopy(out=draft_sb[t][:, W * g : W * (g + 1)], in_=d_banks[n][:])
             if g == 1:
-                nc.sync.dma_start(out=draft[P * t : P * (t + 1), :], in_=draft_sb[t][:])
+                nc.sync.dma_start(out=draft_rows[:, t, :], in_=draft_sb[t][:])
 
         def turn_e(n):
             bank = psum.tile([P, 4, P], F32, name="bank")
@@ -194,103 +175,123 @@ def tile_draft_logit_correction_s9_kernel(tc, x, wd_words, wd_scales, wf, prior,
             et_banks[n] = bank
 
         def weigh_e(n):
-            g, t = divmod(n, 4)
+            t, g = divmod(n, 2)
+            if g == 0:
+                tile = keep.tile([P, 2, P, 4], BF16, name=f"e_g{t}", align_bytes=64)
+                e_g[t] = tile
             nc.vector.tensor_tensor(
-                out=e_g[:, g, P * t : P * (t + 1), :],
-                in0=et_banks[n][:].rearrange("p j t -> p t j"),
+                out=e_g[t][:, g],
+                in0=et_banks[n][:].rearrange("p j r -> p r j"),
                 in1=prior_sb[:, g, :].unsqueeze(1).to_broadcast([P, P, 4]),
                 op=ALU.mult,
             )
 
-        def quant_e(g):
+        def quant_e(t):
+            code = keep.tile([P, 2 * P], U32, name=f"e_q{t}", align_bytes=64)
+            plane = keep.tile([P, 2 * P], U8, name=f"e_s{t}", align_bytes=64)
             nc.vector.quantize_mx(
-                out=e_q[:, g, :].bitcast(E5M2), scales=e_s[:, g, :], in_=e_g[:, g].rearrange("p t k -> p (t k)")
+                out=code[:].bitcast(E5M2), scales=plane[:], in_=e_g[t][:].rearrange("p g r j -> p (g r j)")
             )
+            e_q[t], e_s[t] = code, plane
 
-        acc = {}
+        acc, wide = {}, {}
 
-        def full_mm(m, q):
-            for t in range(4):
-                if m == "f0":
+        def full_mm(block):
+            panel, q = block
+            k = int(panel[1])
+            cols = slice(P * k, P * (k + 1))
+            for t in range(TILES):
+                if panel == PANELS[0]:
                     bank = psum.tile([P, W], F32, name="bank")
                     acc[q, t] = bank
-                k = int(m[1])
-                cols = slice(P * t, P * (t + 1))
-                if m[0] == "f":
-                    lhs, lhs_s = x_q[:, k, cols].bitcast(E4M3), x_s[:, k, cols]
+                if panel[0] == "f":
+                    lhs, lhs_s = x_q[t][:, cols].bitcast(E4M3), x_s[t][:, cols]
                 else:
-                    lhs, lhs_s = e_q[:, k, cols].bitcast(E5M2), e_s[:, k, cols]
+                    lhs, lhs_s = e_q[t][:, cols].bitcast(E5M2), e_s[t][:, cols]
                 nc.tensor.matmul_mx(
                     out=acc[q, t][:],
                     lhsT=lhs,
                     lhsT_scale=lhs_s,
-                    rhs=codes[m, q][:].bitcast(E4M3),
-                    rhs_scale=planes[m, q][:],
-                    start=(m == "f0"),
-                    stop=(m == "c1"),
+                    rhs=codes[block][:].bitcast(E4M3),
+                    rhs_scale=planes[block][:],
+                    start=(panel == PANELS[0]),
+                    stop=(panel == PANELS[-1]),
                 )
 
         def full_out(q, t):
-            tile = work.tile([P, W], F32, name="full_sb", bufs=6)
-            nc.vector.tensor_tensor(out=tile[:], in0=acc[q, t][:], in1=bias_bc[:, W * q : W * (q + 1)], op=ALU.add)
-            nc.sync.dma_start(out=full[P * t : P * (t + 1), W * q : W * (q + 1)], in_=tile[:])
+            half = q % 2
+            if half == 0:
+                tile = work.tile([P, 2 * W], F32, name="full_sb", bufs=8)
+                wide[t] = tile
+            cols = slice(W * half, W * (half + 1))
+            nc.vector.tensor_tensor(
+                out=wide[t][:, cols], in0=acc[q, t][:], in1=bias_bc[:, W * q : W * (q + 1)], op=ALU.add
+            )
+            if q == 1:
+                nc.sync.dma_start(out=full_rows[:, t, : 2 * W], in_=wide[t][:])
+            elif q > 1:
+                nc.sync.dma_start(out=full_rows[:, t, W * q : W * (q + 1)], in_=wide[t][:, cols])
 
-        vcopy, scopy = nc.vector.tensor_copy, nc.scalar.copy
-        head_cut, mid_cut, tail_cut = 256, 128, 352
+        blocks = [(panel, q) for q in range(CHUNKS) for panel in PANELS]
 
-        for i in range(4):
-            turn_x(i)
+        spread_bias(0)
+        turn_x(0)
+        turn_x(1)
+        spread_bias(1)
         copy_x(vcopy, 0)
-        copy_x(scopy, 1)
-        lay("f0", 0, head_cut)
-        copy_x(vcopy, 2)
-        copy_x(scopy, 3)
-        quant("f0", 0)
         quant_x(0)
-        quant_x(1)
-        lay("f1", 0, head_cut)
-        full_mm("f0", 0)
+        copy_x(vcopy, 1)
         draft_mm(0)
         draft_mm(1)
-        quant("f1", 0)
-        mid = [("f0", 1), ("f1", 1), ("c0", 0), ("c1", 0)]
+        quant_x(1)
+        turn_x(2)
+        turn_x(3)
+        copy_x(vcopy, 2)
+        copy_x(vcopy, 3)
+        quant_x(2)
+
+        filler = []
+        for block in blocks[:3]:
+            filler = filler + [
+                lambda block=block: lay(vcopy, block, 0, 256),
+                lambda block=block: lay(vcopy, block, 256, W),
+                lambda block=block: quant(block),
+            ]
+        filler[0]()
         for n in range(8):
             exp(n)
             if n + 2 < 8:
                 draft_mm(n + 2)
             turn_e(n)
-            if n % 2 == 0:
-                lay(*mid[n // 2], mid_cut)
-            elif n > 1:
-                quant(*mid[n // 2 - 1])
-            if n > 0:
-                weigh_e(n - 1)
-            draft_out(scopy, n)
-            if n == 1:
-                full_mm("f1", 0)
-            if n == 5:
-                quant_e(0)
-        weigh_e(7)
-        tail = [("c0", 1), ("c1", 1)] + [(m, q) for q in (2, 3) for m in ("f0", "f1", "c0", "c1")]
-        lay(*tail[0], tail_cut)
-        quant("c1", 0)
-        quant_e(1)
-        full_mm("c0", 0)
-        full_mm("c1", 0)
-        pending = [(0, t) for t in range(4)]
-        outs = [1, 1, 1, 1, 2, 1, 1, 1, 1, 2]
-        for k, unit in enumerate(tail):
-            if k + 1 < len(tail):
-                lay(*tail[k + 1], tail_cut)
-            quant(*unit)
-            for item in pending[: outs[k]]:
-                full_out(*item)
-            pending = pending[outs[k] :]
-            if k == 0:
-                full_mm("f0", 1)
-                full_mm("f1", 1)
-            full_mm(*unit)
-            if unit[0] == "c1":
-                pending += [(unit[1], t) for t in range(4)]
+            draft_out(n)
+            if n == 0:
+                quant_x(3)
+            if n >= 3 and n % 2 == 1:
+                quant_e(n // 2 - 1)
+            if n % 3 == 1:
+                weigh_e(n)
+                filler[n + 1]()
+            else:
+                filler[n + 1]()
+                weigh_e(n)
+        for block in blocks[:2]:
+            full_mm(block)
+
+        pending = []
+        lay(scopy, blocks[3], 0, SCALAR_COLS)
+        lay(vcopy, blocks[3], SCALAR_COLS, W)
+        quant_e(3)
+        full_mm(blocks[2])
+        for b in range(3, len(blocks)):
+            if b + 1 < len(blocks):
+                lay(scopy, blocks[b + 1], 0, SCALAR_COLS)
+                lay(vcopy, blocks[b + 1], SCALAR_COLS, W)
+            quant(blocks[b])
+            if pending:
+                full_out(*pending[0])
+                pending = pending[1:]
+            full_mm(blocks[b])
+            if blocks[b][0] == PANELS[-1]:
+                pending = pending + [(blocks[b][1], t) for t in range(TILES)]
         for item in pending:
             full_out(*item)

@@ -22,7 +22,8 @@ W = 512
 TILES = T // P
 CHUNKS = V // W
 PANELS = ("f0", "f1", "c0", "c1")
-SCALAR_COLS = 336
+SCALAR_COLS = 352
+LAST_COLS = 352
 
 
 def tile_draft_logit_correction_s9_kernel(tc, x, wd_words, wd_scales, wf, prior, c, bias, draft, full):
@@ -38,8 +39,8 @@ def tile_draft_logit_correction_s9_kernel(tc, x, wd_words, wd_scales, wf, prior,
         draft_rows = draft.rearrange("(p i) s -> p i s", i=TILES)
         full_rows = full.rearrange("(p i) v -> p i v", i=TILES)
 
-        bias_col = keep.tile([P, 16], BF16)
-        nc.scalar.dma_start(out=bias_col[:], in_=bias.rearrange("(p i) -> p i", i=16))
+        bias_col = keep.tile([P, 2, 8], BF16)
+        nc.scalar.dma_start(out=bias_col[:], in_=bias.rearrange("(h p i) -> p h i", h=2, i=8))
         prior_sb = keep.tile([P, 2, 4], BF16)
         nc.scalar.dma_start(out=prior_sb[:], in_=prior.rearrange("(g p j) -> p g j", g=2, j=4))
         wd_s = keep.tile([P, 2, S], U8, align_bytes=64)
@@ -74,24 +75,30 @@ def tile_draft_logit_correction_s9_kernel(tc, x, wd_words, wd_scales, wf, prior,
                 out=wd_s[32 * quad : 32 * quad + 4, :, :].bitcast(I32),
                 in_=scales32[:, 4 * quad : 4 * quad + 4, :].rearrange("g r n -> r g n"),
             )
-        load_x(2, 2)
         load_w("f0", 0, 1)
-        for panel in PANELS[1:]:
-            load_w(panel, 0, 2)
+        load_x(2, 2)
         load_w("f0", 1, 1)
+        load_w("f1", 0, 2)
+        load_w("c0", 0, 2)
+        load_w("c1", 0, 2)
         for panel in PANELS:
             load_w(panel, 2, 2)
 
         bias_bc = keep.tile([P, V], BF16)
 
-        def spread_bias(h):
+        bias_banks = {}
+
+        def turn_bias(h):
             bank = psum.tile([P, 4, P], F32, name="bank")
-            words = bias_col[:].bitcast(F32)
+            words = bias_col[:, h, :].bitcast(F32)
             for i in range(4):
-                nc.tensor.transpose(bank[:, i, :], words[:, 4 * h + i : 4 * h + i + 1].to_broadcast([P, P]), ident[:])
+                nc.tensor.transpose(bank[:, i, :], words[:, i : i + 1].to_broadcast([P, P]), ident[:])
+            bias_banks[h] = bank
+
+        def copy_bias(h):
             scopy(
-                out=bias_bc[:].bitcast(F32).rearrange("q (p i) -> q p i", i=8)[:, :, 4 * h : 4 * h + 4],
-                in_=bank[:].rearrange("q i p -> q p i"),
+                out=bias_bc[:, 2 * W * h : 2 * W * (h + 1)].bitcast(F32).rearrange("q (p i) -> q p i", i=4),
+                in_=bias_banks[h][:].rearrange("q i p -> q p i"),
             )
 
         x_banks, x_g, x_q, x_s = {}, {}, {}, {}
@@ -122,7 +129,7 @@ def tile_draft_logit_correction_s9_kernel(tc, x, wd_words, wd_scales, wf, prior,
 
         def lay(copy, block, lo, hi):
             if block not in grouped:
-                tile = work.tile([P, W, 4], BF16, name="grouped", align_bytes=64, bufs=4)
+                tile = work.tile([P, W, 4], BF16, name="grouped", align_bytes=64, bufs=5)
                 grouped[block] = tile
             copy(
                 out=grouped[block][:, lo:hi, :].rearrange("p (c i) j -> p c j i", i=4),
@@ -155,7 +162,7 @@ def tile_draft_logit_correction_s9_kernel(tc, x, wd_words, wd_scales, wf, prior,
             d_banks[n] = bank
 
         def exp(n):
-            rows = work.tile([P, 4, P], F32, name="e_rows", bufs=4)
+            rows = work.tile([P, 4, P], F32, name="e_rows", bufs=6)
             nc.scalar.activation(out=rows[:], in_=d_banks[n][:].rearrange("t (p j) -> t j p", j=4), func=ACT.Exp)
             e_rows[n] = rows
 
@@ -221,7 +228,7 @@ def tile_draft_logit_correction_s9_kernel(tc, x, wd_words, wd_scales, wf, prior,
         def full_out(q, t):
             half = q % 2
             if half == 0:
-                tile = work.tile([P, 2 * W], F32, name="full_sb", bufs=8)
+                tile = work.tile([P, 2 * W], F32, name="full_sb", bufs=7)
                 wide[t] = tile
             cols = slice(W * half, W * (half + 1))
             nc.vector.tensor_tensor(
@@ -232,66 +239,114 @@ def tile_draft_logit_correction_s9_kernel(tc, x, wd_words, wd_scales, wf, prior,
             elif q > 1:
                 nc.sync.dma_start(out=full_rows[:, t, W * q : W * (q + 1)], in_=wide[t][:, cols])
 
-        blocks = [(panel, q) for q in range(CHUNKS) for panel in PANELS]
-
-        spread_bias(0)
+        order = [("f0", 0), ("f0", 1)]
+        order = order + [(panel, q) for q in range(CHUNKS) for panel in PANELS if (panel, q) not in order]
+        turn_bias(0)
+        copy_bias(0)
         turn_x(0)
         turn_x(1)
-        spread_bias(1)
         copy_x(vcopy, 0)
         quant_x(0)
-        copy_x(vcopy, 1)
+        copy_x(scopy, 1)
         draft_mm(0)
         draft_mm(1)
         quant_x(1)
+        lay(vcopy, order[0], 0, W // 2)
+        lay(vcopy, order[0], W // 2, W)
         turn_x(2)
+        draft_mm(2)
+        draft_mm(3)
         turn_x(3)
+        exp(0)
+        draft_out(0)
+        exp(1)
+        draft_out(1)
+        quant(order[0])
         copy_x(vcopy, 2)
-        copy_x(vcopy, 3)
+        lay(vcopy, order[1], 0, W // 2)
         quant_x(2)
-
-        filler = []
-        for block in blocks[:3]:
-            filler = filler + [
-                lambda block=block: lay(vcopy, block, 0, 256),
-                lambda block=block: lay(vcopy, block, 256, W),
-                lambda block=block: quant(block),
-            ]
-        filler[0]()
-        for n in range(8):
-            exp(n)
-            if n + 2 < 8:
-                draft_mm(n + 2)
-            turn_e(n)
-            draft_out(n)
-            if n == 0:
-                quant_x(3)
-            if n >= 3 and n % 2 == 1:
-                quant_e(n // 2 - 1)
-            if n % 3 == 1:
-                weigh_e(n)
-                filler[n + 1]()
-            else:
-                filler[n + 1]()
-                weigh_e(n)
-        for block in blocks[:2]:
-            full_mm(block)
-
-        pending = []
-        lay(scopy, blocks[3], 0, SCALAR_COLS)
-        lay(vcopy, blocks[3], SCALAR_COLS, W)
+        lay(vcopy, order[1], W // 2, W)
+        copy_x(vcopy, 3)
+        quant(order[1])
+        quant_x(3)
+        exp(2)
+        draft_out(2)
+        exp(3)
+        draft_out(3)
+        draft_mm(4)
+        draft_mm(5)
+        turn_e(0)
+        turn_e(1)
+        turn_e(2)
+        draft_mm(6)
+        draft_mm(7)
+        turn_e(3)
+        weigh_e(0)
+        weigh_e(1)
+        lay(vcopy, order[2], 0, W // 2)
+        weigh_e(2)
+        quant_e(0)
+        weigh_e(3)
+        lay(vcopy, order[2], W // 2, W)
+        quant_e(1)
+        exp(4)
+        draft_out(4)
+        turn_e(4)
+        exp(5)
+        draft_out(5)
+        turn_e(5)
+        quant(order[2])
+        weigh_e(4)
+        weigh_e(5)
+        lay(vcopy, order[3], SCALAR_COLS, W)
+        quant_e(2)
+        exp(6)
+        draft_out(6)
+        turn_e(6)
+        turn_bias(1)
+        exp(7)
+        draft_out(7)
+        turn_e(7)
+        copy_bias(1)
+        weigh_e(6)
+        weigh_e(7)
+        lay(scopy, order[3], 0, SCALAR_COLS)
+        lay(vcopy, order[4], SCALAR_COLS, W)
         quant_e(3)
-        full_mm(blocks[2])
-        for b in range(3, len(blocks)):
-            if b + 1 < len(blocks):
-                lay(scopy, blocks[b + 1], 0, SCALAR_COLS)
-                lay(vcopy, blocks[b + 1], SCALAR_COLS, W)
-            quant(blocks[b])
-            if pending:
-                full_out(*pending[0])
-                pending = pending[1:]
-            full_mm(blocks[b])
-            if blocks[b][0] == PANELS[-1]:
-                pending = pending + [(blocks[b][1], t) for t in range(TILES)]
+        lay(scopy, order[4], 0, SCALAR_COLS)
+
+        done = set(order[:3])
+        issued = list(order[:0])
+        pending = []
+
+        def passes():
+            ready = []
+            for q in range(CHUNKS):
+                for panel in PANELS:
+                    if (panel, q) not in done:
+                        return ready
+                    if (panel, q) not in issued:
+                        full_mm((panel, q))
+                        issued.append((panel, q))
+                        if panel == PANELS[-1]:
+                            ready = ready + [(q, t) for t in range(TILES)]
+            return ready
+
+        def cut(b):
+            return LAST_COLS if b >= len(order) - 2 else SCALAR_COLS
+
+        passes()
+        for b in range(3, len(order)):
+            if b + 2 < len(order):
+                lay(scopy, order[b + 2], 0, cut(b + 2))
+            if b + 2 < len(order):
+                lay(vcopy, order[b + 2], cut(b + 2), W)
+            quant(order[b])
+            done.add(order[b])
+            steps_left = len(PANELS) - PANELS.index(order[b][0])
+            count = 2 if len(pending) > steps_left and steps_left <= 2 else 1
+            for item in pending[:count]:
+                full_out(*item)
+            pending = pending[count:] + passes()
         for item in pending:
             full_out(*item)

@@ -40,9 +40,7 @@ def tile_draft_logit_correction_s9_kernel(tc, x, wd_words, wd_scales, wf, prior,
         full_rows = full.rearrange("(p i) v -> p i v", i=TILES)
 
         bias_col = keep.tile([P, 2, 8], BF16)
-        nc.scalar.dma_start(out=bias_col[:], in_=bias.rearrange("(h p i) -> p h i", h=2, i=8))
         prior_sb = keep.tile([P, 2, 4], BF16)
-        nc.scalar.dma_start(out=prior_sb[:], in_=prior.rearrange("(g p j) -> p g j", g=2, j=4))
         wd_s = keep.tile([P, 2, S], U8, align_bytes=64)
         nc.vector.memset(wd_s[:].bitcast(I32), 0)
         ident = keep.tile([P, P], F32)
@@ -67,18 +65,17 @@ def tile_draft_logit_correction_s9_kernel(tc, x, wd_words, wd_scales, wf, prior,
 
         wd_w = keep.tile([P, 2, 2 * S], U8, align_bytes=64)
         load_x(0, 1)
+        scale_rows = wd_scales.bitcast(I32).rearrange("g (quad r) n -> r quad g n", r=4)
+        for r in range(4):
+            nc.sync.dma_start(out=wd_s[r:P:32, :, :].bitcast(I32), in_=scale_rows[r])
         load_x(1, 1)
         nc.sync.dma_start(out=wd_w[:].bitcast(I32), in_=wd_words.bitcast(I32).rearrange("g p n -> p g n"))
-        scales32 = wd_scales.bitcast(I32)
-        for quad in range(4):
-            nc.sync.dma_start(
-                out=wd_s[32 * quad : 32 * quad + 4, :, :].bitcast(I32),
-                in_=scales32[:, 4 * quad : 4 * quad + 4, :].rearrange("g r n -> r g n"),
-            )
         load_w("f0", 0, 1)
         load_x(2, 2)
+        nc.sync.dma_start(out=prior_sb[:], in_=prior.rearrange("(g p j) -> p g j", g=2, j=4))
         load_w("f0", 1, 1)
         load_w("f1", 0, 2)
+        nc.sync.dma_start(out=bias_col[:], in_=bias.rearrange("(h p i) -> p h i", h=2, i=8))
         load_w("c0", 0, 2)
         load_w("c1", 0, 2)
         for panel in PANELS:
@@ -241,8 +238,6 @@ def tile_draft_logit_correction_s9_kernel(tc, x, wd_words, wd_scales, wf, prior,
 
         order = [("f0", 0), ("f0", 1)]
         order = order + [(panel, q) for q in range(CHUNKS) for panel in PANELS if (panel, q) not in order]
-        turn_bias(0)
-        copy_bias(0)
         turn_x(0)
         turn_x(1)
         copy_x(vcopy, 0)
@@ -295,6 +290,7 @@ def tile_draft_logit_correction_s9_kernel(tc, x, wd_words, wd_scales, wf, prior,
         exp(5)
         draft_out(5)
         turn_e(5)
+        turn_bias(0)
         quant(order[2])
         weigh_e(4)
         weigh_e(5)
@@ -307,6 +303,7 @@ def tile_draft_logit_correction_s9_kernel(tc, x, wd_words, wd_scales, wf, prior,
         exp(7)
         draft_out(7)
         turn_e(7)
+        copy_bias(0)
         copy_bias(1)
         weigh_e(6)
         weigh_e(7)

@@ -23,7 +23,8 @@ TILES = T // P
 CHUNKS = V // W
 PANELS = ("f0", "f1", "c0", "c1")
 SCALAR_COLS = 352
-LAST_COLS = 352
+SLOTS = 6
+GPSIMD_COLS = 352
 
 
 def tile_draft_logit_correction_s9_kernel(tc, x, wd_words, wd_scales, wf, prior, c, bias, draft, full):
@@ -124,10 +125,29 @@ def tile_draft_logit_correction_s9_kernel(tc, x, wd_words, wd_scales, wf, prior,
 
         grouped, codes, planes = {}, {}, {}
 
+        idle_slots = list(range(SLOTS))
+        slot = {}
+
+        def take_slot(block, newest):
+            slot[block] = idle_slots[-1] if newest else idle_slots[0]
+            idle_slots.remove(slot[block])
+            tile = keep.tile([P, W, 4], BF16, name=f"grouped{slot[block]}", align_bytes=64)
+            grouped[block] = tile
+
+        def lay_gpsimd(block, hi):
+            take_slot(block, True)
+            nc.gpsimd.tensor_scalar(
+                out=grouped[block][:, :hi, :],
+                in0=raw[block][:, :, :hi].rearrange("p j n -> p n j"),
+                scalar1=1.0,
+                scalar2=0.0,
+                op0=ALU.mult,
+                op1=ALU.add,
+            )
+
         def lay(copy, block, lo, hi):
             if block not in grouped:
-                tile = work.tile([P, W, 4], BF16, name="grouped", align_bytes=64, bufs=5)
-                grouped[block] = tile
+                take_slot(block, False)
             copy(
                 out=grouped[block][:, lo:hi, :].rearrange("p (c i) j -> p c j i", i=4),
                 in_=raw[block][:, :, lo:hi].rearrange("p j (c i) -> p c j i", i=4),
@@ -140,6 +160,7 @@ def tile_draft_logit_correction_s9_kernel(tc, x, wd_words, wd_scales, wf, prior,
                 out=code[:].bitcast(E4M3), scales=plane[:], in_=grouped[block][:].rearrange("p n j -> p (n j)")
             )
             codes[block], planes[block] = code, plane
+            idle_slots.append(slot[block])
 
         d_banks, e_rows, et_banks, e_g, e_q, e_s, draft_sb = {}, {}, {}, {}, {}, {}, {}
 
@@ -198,14 +219,16 @@ def tile_draft_logit_correction_s9_kernel(tc, x, wd_words, wd_scales, wf, prior,
             )
             e_q[t], e_s[t] = code, plane
 
-        acc, wide = {}, {}
+        acc, wide, passes_done = {}, {}, {}
 
         def full_mm(block):
             panel, q = block
             k = int(panel[1])
             cols = slice(P * k, P * (k + 1))
+            nth = passes_done.get(q, 0)
+            passes_done[q] = nth + 1
             for t in range(TILES):
-                if panel == PANELS[0]:
+                if nth == 0:
                     bank = psum.tile([P, W], F32, name="bank")
                     acc[q, t] = bank
                 if panel[0] == "f":
@@ -218,8 +241,8 @@ def tile_draft_logit_correction_s9_kernel(tc, x, wd_words, wd_scales, wf, prior,
                     lhsT_scale=lhs_s,
                     rhs=codes[block][:].bitcast(E4M3),
                     rhs_scale=planes[block][:],
-                    start=(panel == PANELS[0]),
-                    stop=(panel == PANELS[-1]),
+                    start=(nth == 0),
+                    stop=(nth == len(PANELS) - 1),
                 )
 
         def full_out(q, t):
@@ -262,8 +285,9 @@ def tile_draft_logit_correction_s9_kernel(tc, x, wd_words, wd_scales, wf, prior,
         quant_x(2)
         lay(vcopy, order[1], W // 2, W)
         copy_x(vcopy, 3)
-        quant(order[1])
         quant_x(3)
+        quant(order[1])
+        lay_gpsimd(order[2], 352)
         exp(2)
         draft_out(2)
         exp(3)
@@ -272,18 +296,14 @@ def tile_draft_logit_correction_s9_kernel(tc, x, wd_words, wd_scales, wf, prior,
         draft_mm(5)
         turn_e(0)
         turn_e(1)
-        turn_e(2)
         draft_mm(6)
-        draft_mm(7)
+        turn_e(2)
         turn_e(3)
+        draft_mm(7)
         weigh_e(0)
         weigh_e(1)
-        lay(vcopy, order[2], 0, W // 2)
         weigh_e(2)
-        quant_e(0)
         weigh_e(3)
-        lay(vcopy, order[2], W // 2, W)
-        quant_e(1)
         exp(4)
         draft_out(4)
         turn_e(4)
@@ -291,11 +311,11 @@ def tile_draft_logit_correction_s9_kernel(tc, x, wd_words, wd_scales, wf, prior,
         draft_out(5)
         turn_e(5)
         turn_bias(0)
+        quant_e(0)
+        lay(vcopy, order[2], 352, 512)
+        quant_e(1)
         quant(order[2])
-        weigh_e(4)
-        weigh_e(5)
-        lay(vcopy, order[3], SCALAR_COLS, W)
-        quant_e(2)
+        lay_gpsimd(order[3], 352)
         exp(6)
         draft_out(6)
         turn_e(6)
@@ -305,45 +325,70 @@ def tile_draft_logit_correction_s9_kernel(tc, x, wd_words, wd_scales, wf, prior,
         turn_e(7)
         copy_bias(0)
         copy_bias(1)
+        weigh_e(4)
+        weigh_e(5)
         weigh_e(6)
         weigh_e(7)
-        lay(scopy, order[3], 0, SCALAR_COLS)
-        lay(vcopy, order[4], SCALAR_COLS, W)
+        full_mm(order[0])
+        full_mm(order[2])
+        full_mm(order[1])
+        lay(scopy, order[4], 0, 512)
+        quant_e(2)
+        lay(vcopy, order[3], 352, 512)
         quant_e(3)
-        lay(scopy, order[4], 0, SCALAR_COLS)
-
-        done = set(order[:3])
-        issued = list(order[:0])
-        pending = []
-
-        def passes():
-            ready = []
-            for q in range(CHUNKS):
-                for panel in PANELS:
-                    if (panel, q) not in done:
-                        return ready
-                    if (panel, q) not in issued:
-                        full_mm((panel, q))
-                        issued.append((panel, q))
-                        if panel == PANELS[-1]:
-                            ready = ready + [(q, t) for t in range(TILES)]
-            return ready
-
-        def cut(b):
-            return LAST_COLS if b >= len(order) - 2 else SCALAR_COLS
-
-        passes()
-        for b in range(3, len(order)):
-            if b + 2 < len(order):
-                lay(scopy, order[b + 2], 0, cut(b + 2))
-            if b + 2 < len(order):
-                lay(vcopy, order[b + 2], cut(b + 2), W)
-            quant(order[b])
-            done.add(order[b])
-            steps_left = len(PANELS) - PANELS.index(order[b][0])
-            count = 2 if len(pending) > steps_left and steps_left <= 2 else 1
-            for item in pending[:count]:
-                full_out(*item)
-            pending = pending[count:] + passes()
-        for item in pending:
-            full_out(*item)
+        quant(order[3])
+        full_mm(order[3])
+        lay(scopy, order[5], 0, 512)
+        quant(order[4])
+        full_mm(order[4])
+        lay(vcopy, order[6], 0, 512)
+        lay(scopy, order[7], 0, 512)
+        quant(order[5])
+        full_mm(order[5])
+        quant(order[6])
+        lay_gpsimd(order[10], 352)
+        full_mm(order[6])
+        full_out(0, 0)
+        full_out(0, 1)
+        full_out(0, 2)
+        full_out(0, 3)
+        lay(scopy, order[8], 0, 512)
+        quant(order[7])
+        full_mm(order[7])
+        lay(vcopy, order[10], 352, 512)
+        lay(vcopy, order[11], 0, 256)
+        quant(order[8])
+        full_mm(order[8])
+        lay(scopy, order[9], 0, 512)
+        lay(vcopy, order[11], 256, 512)
+        quant(order[10])
+        full_mm(order[10])
+        lay(scopy, order[13], 0, 512)
+        quant(order[9])
+        full_mm(order[9])
+        quant(order[11])
+        lay_gpsimd(order[12], 352)
+        full_mm(order[11])
+        full_out(1, 0)
+        full_out(1, 1)
+        full_out(1, 2)
+        full_out(1, 3)
+        lay(scopy, order[14], 0, 512)
+        quant(order[13])
+        full_mm(order[13])
+        lay(vcopy, order[12], 352, 512)
+        full_out(2, 0)
+        lay(scopy, order[15], 0, 512)
+        quant(order[12])
+        full_mm(order[12])
+        full_out(2, 1)
+        quant(order[14])
+        full_mm(order[14])
+        full_out(2, 2)
+        quant(order[15])
+        full_mm(order[15])
+        full_out(2, 3)
+        full_out(3, 0)
+        full_out(3, 1)
+        full_out(3, 2)
+        full_out(3, 3)

@@ -184,12 +184,12 @@ def tile_draft_logit_correction_s9_kernel(tc, x, wd_words, wd_scales, wf, prior,
             nc.scalar.activation(out=rows[:], in_=d_banks[n][:].rearrange("t (p j) -> t j p", j=4), func=ACT.Exp)
             e_rows[n] = rows
 
-        def draft_out(n):
+        def draft_out(copy, n):
             t, g = divmod(n, 2)
             if g == 0:
                 tile = keep.tile([P, S], F32, name=f"draft_sb{t}")
                 draft_sb[t] = tile
-            scopy(out=draft_sb[t][:, W * g : W * (g + 1)], in_=d_banks[n][:])
+            copy(out=draft_sb[t][:, W * g : W * (g + 1)], in_=d_banks[n][:])
             if g == 1:
                 nc.sync.dma_start(out=draft_rows[:, t, :], in_=draft_sb[t][:])
 
@@ -219,15 +219,15 @@ def tile_draft_logit_correction_s9_kernel(tc, x, wd_words, wd_scales, wf, prior,
             )
             e_q[t], e_s[t] = code, plane
 
-        acc, wide, passes_done = {}, {}, {}
+        acc, passes_done = {}, {}
 
-        def full_mm(block):
+        def full_mm(block, tiles=range(TILES)):
             panel, q = block
             k = int(panel[1])
             cols = slice(P * k, P * (k + 1))
-            nth = passes_done.get(q, 0)
-            passes_done[q] = nth + 1
-            for t in range(TILES):
+            for t in tiles:
+                nth = passes_done.get((q, t), 0)
+                passes_done[q, t] = nth + 1
                 if nth == 0:
                     bank = psum.tile([P, W], F32, name="bank")
                     acc[q, t] = bank
@@ -245,19 +245,11 @@ def tile_draft_logit_correction_s9_kernel(tc, x, wd_words, wd_scales, wf, prior,
                     stop=(nth == len(PANELS) - 1),
                 )
 
-        def full_out(q, t):
-            half = q % 2
-            if half == 0:
-                tile = work.tile([P, 2 * W], F32, name="full_sb", bufs=7)
-                wide[t] = tile
-            cols = slice(W * half, W * (half + 1))
-            nc.vector.tensor_tensor(
-                out=wide[t][:, cols], in0=acc[q, t][:], in1=bias_bc[:, W * q : W * (q + 1)], op=ALU.add
-            )
-            if q == 1:
-                nc.sync.dma_start(out=full_rows[:, t, : 2 * W], in_=wide[t][:])
-            elif q > 1:
-                nc.sync.dma_start(out=full_rows[:, t, W * q : W * (q + 1)], in_=wide[t][:, cols])
+        def full_out(q, t, lo=0, hi=W):
+            tile = work.tile([P, hi - lo], F32, name="full_sb", bufs=10)
+            cols = slice(W * q + lo, W * q + hi)
+            nc.vector.tensor_tensor(out=tile[:], in0=acc[q, t][:, lo:hi], in1=bias_bc[:, cols], op=ALU.add)
+            nc.sync.dma_start(out=full_rows[:, t, cols], in_=tile[:])
 
         order = [("f0", 0), ("f0", 1)]
         order = order + [(panel, q) for q in range(CHUNKS) for panel in PANELS if (panel, q) not in order]
@@ -265,68 +257,67 @@ def tile_draft_logit_correction_s9_kernel(tc, x, wd_words, wd_scales, wf, prior,
         turn_x(1)
         copy_x(vcopy, 0)
         quant_x(0)
-        copy_x(scopy, 1)
+        copy_x(vcopy, 1)
         draft_mm(0)
         draft_mm(1)
         quant_x(1)
-        lay(vcopy, order[0], 0, W // 2)
-        lay(vcopy, order[0], W // 2, W)
+        lay(scopy, order[0], 0, 96)
+        lay(vcopy, order[0], 96, 512)
         turn_x(2)
+        turn_x(3)
         draft_mm(2)
         draft_mm(3)
-        turn_x(3)
         exp(0)
-        draft_out(0)
+        draft_out(vcopy, 0)
         exp(1)
-        draft_out(1)
         quant(order[0])
-        copy_x(vcopy, 2)
-        lay(vcopy, order[1], 0, W // 2)
-        quant_x(2)
-        lay(vcopy, order[1], W // 2, W)
-        copy_x(vcopy, 3)
-        quant_x(3)
-        quant(order[1])
-        lay_gpsimd(order[2], 352)
-        exp(2)
-        draft_out(2)
-        exp(3)
-        draft_out(3)
-        draft_mm(4)
-        draft_mm(5)
+        draft_out(scopy, 1)
+        copy_x(scopy, 2)
+        lay(vcopy, order[1], 0, 512)
+        copy_x(scopy, 3)
         turn_e(0)
         turn_e(1)
-        draft_mm(6)
+        quant_x(2)
+        quant_x(3)
+        exp(2)
+        exp(3)
+        draft_mm(4)
+        draft_mm(5)
         turn_e(2)
         turn_e(3)
-        draft_mm(7)
+        quant(order[1])
+        lay_gpsimd(order[2], 512)
+        draft_out(scopy, 2)
         weigh_e(0)
         weigh_e(1)
+        draft_out(vcopy, 3)
         weigh_e(2)
         weigh_e(3)
+        draft_mm(6)
+        draft_mm(7)
         exp(4)
-        draft_out(4)
+        draft_out(scopy, 4)
         turn_e(4)
         exp(5)
-        draft_out(5)
+        draft_out(scopy, 5)
         turn_e(5)
         turn_bias(0)
-        quant_e(0)
-        lay(vcopy, order[2], 352, 512)
-        quant_e(1)
-        quant(order[2])
-        lay_gpsimd(order[3], 352)
         exp(6)
-        draft_out(6)
+        exp(7)
         turn_e(6)
         turn_bias(1)
-        exp(7)
-        draft_out(7)
         turn_e(7)
+        quant_e(0)
+        lay(vcopy, order[5], 0, 512)
+        quant_e(1)
+        quant(order[2])
+        lay_gpsimd(order[3], 512)
+        draft_out(scopy, 6)
         copy_bias(0)
         copy_bias(1)
         weigh_e(4)
         weigh_e(5)
+        draft_out(vcopy, 7)
         weigh_e(6)
         weigh_e(7)
         full_mm(order[0])
@@ -334,59 +325,63 @@ def tile_draft_logit_correction_s9_kernel(tc, x, wd_words, wd_scales, wf, prior,
         full_mm(order[1])
         lay(scopy, order[4], 0, 512)
         quant_e(2)
-        lay(vcopy, order[3], 352, 512)
+        lay(vcopy, order[7], 0, 256)
         quant_e(3)
+        lay(scopy, order[6], 0, 512)
         quant(order[3])
         full_mm(order[3])
-        lay(scopy, order[5], 0, 512)
         quant(order[4])
         full_mm(order[4])
-        lay(vcopy, order[6], 0, 512)
-        lay(scopy, order[7], 0, 512)
+        lay(scopy, order[7], 256, 512)
         quant(order[5])
         full_mm(order[5])
+        lay(scopy, order[8], 0, 512)
         quant(order[6])
-        lay_gpsimd(order[10], 352)
         full_mm(order[6])
+        quant(order[7])
+        lay_gpsimd(order[10], 352)
+        full_mm(order[7])
         full_out(0, 0)
         full_out(0, 1)
         full_out(0, 2)
         full_out(0, 3)
-        lay(scopy, order[8], 0, 512)
-        quant(order[7])
-        full_mm(order[7])
-        lay(vcopy, order[10], 352, 512)
-        lay(vcopy, order[11], 0, 256)
+        lay(scopy, order[9], 0, 512)
         quant(order[8])
         full_mm(order[8])
-        lay(scopy, order[9], 0, 512)
-        lay(vcopy, order[11], 256, 512)
-        quant(order[10])
-        full_mm(order[10])
-        lay(scopy, order[13], 0, 512)
+        lay(vcopy, order[11], 0, 512)
+        lay(scopy, order[10], 352, 512)
         quant(order[9])
         full_mm(order[9])
+        lay(scopy, order[13], 0, 512)
+        quant(order[10])
+        full_mm(order[10])
         quant(order[11])
-        lay_gpsimd(order[12], 352)
+        lay_gpsimd(order[12], 448)
         full_mm(order[11])
+        lay(scopy, order[12], 448, 512)
         full_out(1, 0)
         full_out(1, 1)
         full_out(1, 2)
         full_out(1, 3)
+        full_out(2, 0)
         lay(scopy, order[14], 0, 512)
         quant(order[13])
         full_mm(order[13])
-        lay(vcopy, order[12], 352, 512)
-        full_out(2, 0)
-        lay(scopy, order[15], 0, 512)
         quant(order[12])
         full_mm(order[12])
+        lay(scopy, order[15], 0, 512)
         full_out(2, 1)
         quant(order[14])
-        full_mm(order[14])
         full_out(2, 2)
         quant(order[15])
-        full_mm(order[15])
+        full_mm(order[14], [0])
+        full_mm(order[15], [0])
+        full_mm(order[14], [1])
+        full_mm(order[15], [1])
+        full_mm(order[14], [2])
+        full_mm(order[15], [2])
+        full_mm(order[14], [3])
+        full_mm(order[15], [3])
         full_out(2, 3)
         full_out(3, 0)
         full_out(3, 1)

@@ -78,9 +78,10 @@ def tile_draft_logit_correction_s9_kernel(tc, x, wd_words, wd_scales, wf, prior,
         load_w("f1", 0, 2)
         nc.sync.dma_start(out=bias_col[:], in_=bias.rearrange("(h p i) -> p h i", h=2, i=8))
         load_w("c0", 0, 2)
-        load_w("c1", 0, 2)
-        for panel in PANELS:
-            load_w(panel, 2, 2)
+        load_w("c1", 0, 4)
+        load_w("f0", 2, 2)
+        load_w("f1", 2, 2)
+        load_w("c0", 2, 2)
 
         bias_bc = keep.tile([P, V], BF16)
 
@@ -153,6 +154,18 @@ def tile_draft_logit_correction_s9_kernel(tc, x, wd_words, wd_scales, wf, prior,
                 in_=raw[block][:, :, lo:hi].rearrange("p j (c i) -> p c j i", i=4),
             )
 
+        def quant_half(block, h):
+            if h == 0:
+                code = keep.tile([P, W], U32, name=f"code_{block[0]}_{block[1]}", align_bytes=64)
+                plane = keep.tile([P, W], U8, name=f"plane_{block[0]}_{block[1]}", align_bytes=64)
+                codes[block], planes[block] = code, plane
+            cols = slice(h * W // 2, (h + 1) * W // 2)
+            nc.vector.quantize_mx(
+                out=codes[block][:, cols].bitcast(E4M3),
+                scales=planes[block][:, cols],
+                in_=grouped[block][:, cols, :].rearrange("p n j -> p (n j)"),
+            )
+
         def quant(block):
             code = keep.tile([P, W], U32, name=f"code_{block[0]}_{block[1]}", align_bytes=64)
             plane = keep.tile([P, W], U8, name=f"plane_{block[0]}_{block[1]}", align_bytes=64)
@@ -163,6 +176,8 @@ def tile_draft_logit_correction_s9_kernel(tc, x, wd_words, wd_scales, wf, prior,
             idle_slots.append(slot[block])
 
         d_banks, e_rows, et_banks, e_g, e_q, e_s, draft_sb = {}, {}, {}, {}, {}, {}, {}
+
+        drafts_done = []
 
         def draft_mm(n):
             t, g = divmod(n, 2)
@@ -186,12 +201,17 @@ def tile_draft_logit_correction_s9_kernel(tc, x, wd_words, wd_scales, wf, prior,
 
         def draft_out(copy, n):
             t, g = divmod(n, 2)
-            if g == 0:
-                tile = keep.tile([P, S], F32, name=f"draft_sb{t}")
-                draft_sb[t] = tile
-            copy(out=draft_sb[t][:, W * g : W * (g + 1)], in_=d_banks[n][:])
-            if g == 1:
-                nc.sync.dma_start(out=draft_rows[:, t, :], in_=draft_sb[t][:])
+            pair = t // 2
+            if pair not in draft_sb:
+                tile = keep.tile([P, 4, W], F32, name=f"draft_sb{pair}")
+                draft_sb[pair] = tile
+            copy(out=draft_sb[pair][:, n % 4, :], in_=d_banks[n][:])
+            drafts_done.append(n)
+            if all(4 * pair + i in drafts_done for i in range(4)):
+                nc.sync.dma_start(
+                    out=draft_rows[:, 2 * pair : 2 * pair + 2, :].rearrange("p i s -> p (i s)"),
+                    in_=draft_sb[pair][:].rearrange("p n s -> p (n s)"),
+                )
 
         def turn_e(n):
             bank = psum.tile([P, 4, P], F32, name="bank")
@@ -245,14 +265,28 @@ def tile_draft_logit_correction_s9_kernel(tc, x, wd_words, wd_scales, wf, prior,
                     stop=(nth == len(PANELS) - 1),
                 )
 
+        def half_mm(block, h, t):
+            panel, q = block
+            k = int(panel[1])
+            cols = slice(h * W // 2, (h + 1) * W // 2)
+            nc.tensor.matmul_mx(
+                out=acc[q, t][:, cols],
+                lhsT=x_q[t][:, P * k : P * (k + 1)].bitcast(E4M3),
+                lhsT_scale=x_s[t][:, P * k : P * (k + 1)],
+                rhs=codes[block][:, cols].bitcast(E4M3),
+                rhs_scale=planes[block][:, cols],
+                start=False,
+                stop=(h == 1),
+            )
+
         def full_out(q, t, lo=0, hi=W):
             tile = work.tile([P, hi - lo], F32, name="full_sb", bufs=10)
             cols = slice(W * q + lo, W * q + hi)
             nc.vector.tensor_tensor(out=tile[:], in0=acc[q, t][:, lo:hi], in1=bias_bc[:, cols], op=ALU.add)
             nc.sync.dma_start(out=full_rows[:, t, cols], in_=tile[:])
 
-        order = [("f0", 0), ("f0", 1)]
-        order = order + [(panel, q) for q in range(CHUNKS) for panel in PANELS if (panel, q) not in order]
+        order = [("f0", 0), ("f0", 1), ("f1", 0), ("c0", 0), ("c1", 0), ("f1", 1), ("c0", 1), ("c1", 1)]
+        order = order + [(panel, 2) for panel in PANELS] + [(panel, 3) for panel in ("c0", "c1", "f0", "f1")]
         turn_x(0)
         turn_x(1)
         copy_x(vcopy, 0)
@@ -323,23 +357,23 @@ def tile_draft_logit_correction_s9_kernel(tc, x, wd_words, wd_scales, wf, prior,
         full_mm(order[0])
         full_mm(order[2])
         full_mm(order[1])
-        lay(scopy, order[4], 0, 512)
-        quant_e(2)
-        lay(vcopy, order[7], 0, 256)
-        quant_e(3)
         lay(scopy, order[6], 0, 512)
+        quant_e(2)
+        lay(vcopy, order[7], 0, 320)
+        quant_e(3)
+        lay(scopy, order[4], 0, 512)
         quant(order[3])
         full_mm(order[3])
+        quant(order[6])
+        lay(scopy, order[7], 320, 512)
         quant(order[4])
         full_mm(order[4])
-        lay(scopy, order[7], 256, 512)
+        full_mm(order[6])
         quant(order[5])
         full_mm(order[5])
         lay(scopy, order[8], 0, 512)
-        quant(order[6])
-        full_mm(order[6])
         quant(order[7])
-        lay_gpsimd(order[10], 352)
+        lay_gpsimd(order[11], 352)
         full_mm(order[7])
         full_out(0, 0)
         full_out(0, 1)
@@ -348,16 +382,16 @@ def tile_draft_logit_correction_s9_kernel(tc, x, wd_words, wd_scales, wf, prior,
         lay(scopy, order[9], 0, 512)
         quant(order[8])
         full_mm(order[8])
-        lay(vcopy, order[11], 0, 512)
-        lay(scopy, order[10], 352, 512)
+        lay(vcopy, order[10], 0, 512)
+        lay(scopy, order[11], 352, 512)
         quant(order[9])
         full_mm(order[9])
         lay(scopy, order[13], 0, 512)
-        quant(order[10])
-        full_mm(order[10])
         quant(order[11])
-        lay_gpsimd(order[12], 448)
         full_mm(order[11])
+        quant(order[10])
+        lay_gpsimd(order[12], 448)
+        full_mm(order[10])
         lay(scopy, order[12], 448, 512)
         full_out(1, 0)
         full_out(1, 1)
@@ -369,19 +403,25 @@ def tile_draft_logit_correction_s9_kernel(tc, x, wd_words, wd_scales, wf, prior,
         full_mm(order[13])
         quant(order[12])
         full_mm(order[12])
-        lay(scopy, order[15], 0, 512)
+        lay(scopy, order[15], 0, 256)
+        lay(scopy, order[15], 256, 512)
         full_out(2, 1)
         quant(order[14])
         full_out(2, 2)
-        quant(order[15])
+        quant_half(order[15], 0)
+        quant_half(order[15], 1)
         full_mm(order[14], [0])
-        full_mm(order[15], [0])
+        half_mm(order[15], 0, 0)
+        half_mm(order[15], 1, 0)
         full_mm(order[14], [1])
-        full_mm(order[15], [1])
+        half_mm(order[15], 0, 1)
+        half_mm(order[15], 1, 1)
         full_mm(order[14], [2])
-        full_mm(order[15], [2])
+        half_mm(order[15], 0, 2)
+        half_mm(order[15], 1, 2)
         full_mm(order[14], [3])
-        full_mm(order[15], [3])
+        half_mm(order[15], 0, 3)
+        half_mm(order[15], 1, 3)
         full_out(2, 3)
         full_out(3, 0)
         full_out(3, 1)

@@ -73,8 +73,8 @@ def tile_draft_logit_correction_s9_kernel(tc, x, wd_words, wd_scales, wf, prior,
         nc.sync.dma_start(out=wd_w[:].bitcast(I32), in_=wd_words.bitcast(I32).rearrange("g p n -> p g n"))
         load_w("f0", 0, 1)
         load_x(2, 2)
-        nc.sync.dma_start(out=prior_sb[:], in_=prior.rearrange("(g p j) -> p g j", g=2, j=4))
         load_w("f0", 1, 1)
+        nc.sync.dma_start(out=prior_sb[:], in_=prior.rearrange("(g p j) -> p g j", g=2, j=4))
         load_w("f1", 0, 2)
         nc.sync.dma_start(out=bias_col[:], in_=bias.rearrange("(h p i) -> p h i", h=2, i=8))
         load_w("c0", 0, 2)
@@ -320,7 +320,7 @@ def tile_draft_logit_correction_s9_kernel(tc, x, wd_words, wd_scales, wf, prior,
         turn_e(2)
         turn_e(3)
         quant(order[1])
-        lay_gpsimd(order[2], 512)
+        lay_gpsimd(order[2], 480)
         draft_out(scopy, 2)
         weigh_e(0)
         weigh_e(1)
@@ -342,10 +342,11 @@ def tile_draft_logit_correction_s9_kernel(tc, x, wd_words, wd_scales, wf, prior,
         turn_bias(1)
         turn_e(7)
         quant_e(0)
+        lay(vcopy, order[2], 480, 512)
         lay(vcopy, order[5], 0, 512)
         quant_e(1)
         quant(order[2])
-        lay_gpsimd(order[3], 512)
+        lay_gpsimd(order[3], 480)
         draft_out(scopy, 6)
         copy_bias(0)
         copy_bias(1)
@@ -359,13 +360,14 @@ def tile_draft_logit_correction_s9_kernel(tc, x, wd_words, wd_scales, wf, prior,
         full_mm(order[1])
         lay(scopy, order[6], 0, 512)
         quant_e(2)
-        lay(vcopy, order[7], 0, 320)
+        lay(vcopy, order[3], 480, 512)
+        lay(vcopy, order[7], 0, 160)
         quant_e(3)
         lay(scopy, order[4], 0, 512)
         quant(order[3])
         full_mm(order[3])
         quant(order[6])
-        lay(scopy, order[7], 320, 512)
+        lay(scopy, order[7], 160, 512)
         quant(order[4])
         full_mm(order[4])
         full_mm(order[6])

@@ -150,8 +150,8 @@ def tile_draft_logit_correction_s9_kernel(tc, x, wd_words, wd_scales, wf, prior,
             if block not in grouped:
                 take_slot(block, False)
             copy(
-                out=grouped[block][:, lo:hi, :].rearrange("p (c i) j -> p c j i", i=4),
-                in_=raw[block][:, :, lo:hi].rearrange("p j (c i) -> p c j i", i=4),
+                out=grouped[block][:, lo:hi, :].rearrange("p (c i) (h e) -> p c h i e", i=4, e=2),
+                in_=raw[block][:, :, lo:hi].rearrange("p (h e) (c i) -> p c h i e", i=4, e=2),
             )
 
         def quant_half(block, h):

@@ -361,13 +361,13 @@ def tile_draft_logit_correction_s9_kernel(tc, x, wd_words, wd_scales, wf, prior,
         lay(scopy, order[6], 0, 512)
         quant_e(2)
         lay(vcopy, order[3], 480, 512)
-        lay(vcopy, order[7], 0, 160)
+        lay(vcopy, order[7], 0, 224)
         quant_e(3)
         lay(scopy, order[4], 0, 512)
         quant(order[3])
         full_mm(order[3])
         quant(order[6])
-        lay(scopy, order[7], 160, 512)
+        lay(scopy, order[7], 224, 512)
         quant(order[4])
         full_mm(order[4])
         full_mm(order[6])

@@ -22,9 +22,7 @@ W = 512
 TILES = T // P
 CHUNKS = V // W
 PANELS = ("f0", "f1", "c0", "c1")
-SCALAR_COLS = 352
-SLOTS = 6
-GPSIMD_COLS = 352
+ACC_BANKS = (2, 3, 6, 7, 4, 5, 0, 1)
 
 
 def tile_draft_logit_correction_s9_kernel(tc, x, wd_words, wd_scales, wf, prior, c, bias, draft, full):
@@ -32,7 +30,7 @@ def tile_draft_logit_correction_s9_kernel(tc, x, wd_words, wd_scales, wf, prior,
     with ExitStack() as ctx:
         keep = ctx.enter_context(tc.tile_pool(name="keep", bufs=1))
         work = ctx.enter_context(tc.tile_pool(name="work", bufs=2))
-        psum = ctx.enter_context(tc.psum_pool(name="psum", bufs=8))
+        psum = ctx.enter_context(tc.psum_pool(name="psum", bufs=1))
         ctx.enter_context(tc.manual_schedule())
         vcopy, scopy = nc.vector.tensor_copy, nc.scalar.copy
 
@@ -40,14 +38,14 @@ def tile_draft_logit_correction_s9_kernel(tc, x, wd_words, wd_scales, wf, prior,
         draft_rows = draft.rearrange("(p i) s -> p i s", i=TILES)
         full_rows = full.rearrange("(p i) v -> p i v", i=TILES)
 
-        bias_col = keep.tile([P, 2, 8], BF16)
-        prior_sb = keep.tile([P, 2, 4], BF16)
-        wd_s = keep.tile([P, 2, S], U8, align_bytes=64)
+        bias_col = keep.tile([P, 16], BF16, name="bias_col")
+        prior_sb = keep.tile([P, 2, 4], BF16, name="prior_sb")
+        wd_s = keep.tile([P, 2, S], U8, name="wd_s", align_bytes=64)
         nc.vector.memset(wd_s[:].bitcast(I32), 0)
-        ident = keep.tile([P, P], F32)
+        ident = keep.tile([P, P], F32, name="ident")
         make_identity(nc, ident[:])
 
-        x_sb, raw = {}, {}
+        x_sb, raw, wd_w = {}, {}, {}
 
         def load_x(first, count):
             tile = keep.tile([P, count * D], BF16, name=f"x_sb{first}")
@@ -64,54 +62,55 @@ def tile_draft_logit_correction_s9_kernel(tc, x, wd_words, wd_scales, wf, prior,
             for i in range(count):
                 raw[panel, first + i] = tile[:, :, W * i : W * (i + 1)]
 
-        wd_w = keep.tile([P, 2, 2 * S], U8, align_bytes=64)
-        load_x(0, 1)
-        scale_rows = wd_scales.bitcast(I32).rearrange("g (quad r) n -> r quad g n", r=4)
-        for r in range(4):
-            nc.sync.dma_start(out=wd_s[r:P:32, :, :].bitcast(I32), in_=scale_rows[r])
-        load_x(1, 1)
-        nc.sync.dma_start(out=wd_w[:].bitcast(I32), in_=wd_words.bitcast(I32).rearrange("g p n -> p g n"))
-        load_w("f0", 0, 1)
-        load_x(2, 2)
-        load_w("f0", 1, 1)
-        nc.sync.dma_start(out=prior_sb[:], in_=prior.rearrange("(g p j) -> p g j", g=2, j=4))
-        load_w("f1", 0, 2)
-        nc.sync.dma_start(out=bias_col[:], in_=bias.rearrange("(h p i) -> p h i", h=2, i=8))
-        load_w("c0", 0, 2)
-        load_w("c1", 0, 4)
-        load_w("f0", 2, 2)
-        load_w("f1", 2, 2)
-        load_w("c0", 2, 2)
+        def load_wd(first, count):
+            tile = keep.tile([P, 2, 2 * W * count], U8, name=f"wd_w{first}", align_bytes=64)
+            words = wd_words.bitcast(I32).rearrange("g p n -> p g n")
+            nc.sync.dma_start(out=tile[:].bitcast(I32), in_=words[:, :, W // 2 * first : W // 2 * (first + count)])
+            for i in range(count):
+                wd_w[first + i] = tile[:, :, 2 * W * i : 2 * W * (i + 1)]
 
-        bias_bc = keep.tile([P, V], BF16)
+        def load_scales():
+            scale_rows = wd_scales.bitcast(I32).rearrange("g (quad r) n -> r quad g n", r=4)
+            for r in range(4):
+                nc.sync.dma_start(out=wd_s[r:P:32, :, :].bitcast(I32), in_=scale_rows[r])
 
+        def load_prior():
+            nc.sync.dma_start(out=prior_sb[:], in_=prior.rearrange("(g p j) -> p g j", g=2, j=4))
+
+        def load_bias():
+            nc.sync.dma_start(out=bias_col[:], in_=bias.rearrange("(p i) -> p i", i=16))
+
+        def bank_tile(b, shape):
+            return psum.tile(shape, F32, name=f"bank{b}")
+
+        bias_bc = keep.tile([P, V], BF16, name="bias_bc")
         bias_banks = {}
 
-        def turn_bias(h):
-            bank = psum.tile([P, 4, P], F32, name="bank")
-            words = bias_col[:, h, :].bitcast(F32)
+        def turn_bias(h, b):
+            bank = bank_tile(b, [P, 4, P])
+            words = bias_col[:].bitcast(F32)
             for i in range(4):
-                nc.tensor.transpose(bank[:, i, :], words[:, i : i + 1].to_broadcast([P, P]), ident[:])
+                nc.tensor.transpose(bank[:, i, :], words[:, 4 * h + i : 4 * h + i + 1].to_broadcast([P, P]), ident[:])
             bias_banks[h] = bank
 
         def copy_bias(h):
             scopy(
-                out=bias_bc[:, 2 * W * h : 2 * W * (h + 1)].bitcast(F32).rearrange("q (p i) -> q p i", i=4),
+                out=bias_bc[:].bitcast(F32).rearrange("q (p h i) -> q h p i", h=2, i=4)[:, h],
                 in_=bias_banks[h][:].rearrange("q i p -> q p i"),
             )
 
         x_banks, x_g, x_q, x_s = {}, {}, {}, {}
 
-        def turn_x(t):
-            bank = psum.tile([P, 4, P], F32, name="bank")
+        def turn_x(t, b):
+            bank = bank_tile(b, [P, 4, P])
             words = x_sb[t].bitcast(F32)
             for g in range(2):
                 for u in range(2):
                     nc.tensor.transpose(bank[:, 2 * g + u, :], words[:, 256 * g + u : 256 * (g + 1) : 2], ident[:])
             x_banks[t] = bank
 
-        def copy_x(copy, t):
-            tile = keep.tile([P, 2 * P * 4], BF16, name=f"x_g{t}", align_bytes=64)
+        def copy_x(copy, t, slot):
+            tile = keep.tile([P, 2 * P * 4], BF16, name=f"stage{slot}", align_bytes=64)
             copy(
                 out=tile[:].bitcast(F32).rearrange("p (g r u) -> p g r u", g=2, u=2),
                 in_=x_banks[t][:].rearrange("p (g u) r -> p g r u", g=2),
@@ -126,20 +125,13 @@ def tile_draft_logit_correction_s9_kernel(tc, x, wd_words, wd_scales, wf, prior,
 
         grouped, codes, planes = {}, {}, {}
 
-        idle_slots = list(range(SLOTS))
-        slot = {}
+        def take_slot(block, slot):
+            grouped[block] = keep.tile([P, W, 4], BF16, name=f"stage{slot}", align_bytes=64)
 
-        def take_slot(block, newest):
-            slot[block] = idle_slots[-1] if newest else idle_slots[0]
-            idle_slots.remove(slot[block])
-            tile = keep.tile([P, W, 4], BF16, name=f"grouped{slot[block]}", align_bytes=64)
-            grouped[block] = tile
-
-        def lay_gpsimd(block, hi):
-            take_slot(block, True)
+        def lay_gpsimd(block, lo, hi):
             nc.gpsimd.tensor_scalar(
-                out=grouped[block][:, :hi, :],
-                in0=raw[block][:, :, :hi].rearrange("p j n -> p n j"),
+                out=grouped[block][:, lo:hi, :],
+                in0=raw[block][:, :, lo:hi].rearrange("p j n -> p n j"),
                 scalar1=1.0,
                 scalar2=0.0,
                 op0=ALU.mult,
@@ -147,47 +139,33 @@ def tile_draft_logit_correction_s9_kernel(tc, x, wd_words, wd_scales, wf, prior,
             )
 
         def lay(copy, block, lo, hi):
-            if block not in grouped:
-                take_slot(block, False)
             copy(
                 out=grouped[block][:, lo:hi, :].rearrange("p (c i) (h e) -> p c h i e", i=4, e=2),
                 in_=raw[block][:, :, lo:hi].rearrange("p (h e) (c i) -> p c h i e", i=4, e=2),
             )
 
-        def quant_half(block, h):
-            if h == 0:
-                code = keep.tile([P, W], U32, name=f"code_{block[0]}_{block[1]}", align_bytes=64)
-                plane = keep.tile([P, W], U8, name=f"plane_{block[0]}_{block[1]}", align_bytes=64)
-                codes[block], planes[block] = code, plane
-            cols = slice(h * W // 2, (h + 1) * W // 2)
+        def quant(block, lo=0, hi=W):
+            if lo == 0:
+                codes[block] = keep.tile([P, W], U32, name=f"code_{block[0]}_{block[1]}", align_bytes=64)
+                planes[block] = keep.tile([P, W], U8, name=f"plane_{block[0]}_{block[1]}", align_bytes=64)
             nc.vector.quantize_mx(
-                out=codes[block][:, cols].bitcast(E4M3),
-                scales=planes[block][:, cols],
-                in_=grouped[block][:, cols, :].rearrange("p n j -> p (n j)"),
+                out=codes[block][:, lo:hi].bitcast(E4M3),
+                scales=planes[block][:, lo:hi],
+                in_=grouped[block][:, lo:hi, :].rearrange("p n j -> p (n j)"),
             )
-
-        def quant(block):
-            code = keep.tile([P, W], U32, name=f"code_{block[0]}_{block[1]}", align_bytes=64)
-            plane = keep.tile([P, W], U8, name=f"plane_{block[0]}_{block[1]}", align_bytes=64)
-            nc.vector.quantize_mx(
-                out=code[:].bitcast(E4M3), scales=plane[:], in_=grouped[block][:].rearrange("p n j -> p (n j)")
-            )
-            codes[block], planes[block] = code, plane
-            idle_slots.append(slot[block])
 
         d_banks, e_rows, et_banks, e_g, e_q, e_s, draft_sb = {}, {}, {}, {}, {}, {}, {}
-
         drafts_done = []
 
-        def draft_mm(n):
+        def draft_mm(n, b):
             t, g = divmod(n, 2)
-            bank = psum.tile([P, W], F32, name="bank")
+            bank = bank_tile(b, [P, W])
             for k in range(2):
                 nc.tensor.matmul_mx(
                     out=bank[:],
                     lhsT=x_q[t][:, P * k : P * (k + 1)].bitcast(E4M3),
                     lhsT_scale=x_s[t][:, P * k : P * (k + 1)],
-                    rhs=wd_w[:, k, 2 * W * g : 2 * W * (g + 1)].bitcast(E2M1),
+                    rhs=wd_w[g][:, k, :].bitcast(E2M1),
                     rhs_scale=wd_s[:, k, W * g : W * (g + 1)],
                     start=(k == 0),
                     stop=(k == 1),
@@ -195,16 +173,14 @@ def tile_draft_logit_correction_s9_kernel(tc, x, wd_words, wd_scales, wf, prior,
             d_banks[n] = bank
 
         def exp(n):
-            rows = work.tile([P, 4, P], F32, name="e_rows", bufs=6)
+            rows = work.tile([P, 4, P], F32, name="e_rows", bufs=4)
             nc.scalar.activation(out=rows[:], in_=d_banks[n][:].rearrange("t (p j) -> t j p", j=4), func=ACT.Exp)
             e_rows[n] = rows
 
         def draft_out(copy, n):
-            t, g = divmod(n, 2)
-            pair = t // 2
+            pair = n // 4
             if pair not in draft_sb:
-                tile = keep.tile([P, 4, W], F32, name=f"draft_sb{pair}")
-                draft_sb[pair] = tile
+                draft_sb[pair] = keep.tile([P, 4, W], F32, name=f"draft_sb{pair}")
             copy(out=draft_sb[pair][:, n % 4, :], in_=d_banks[n][:])
             drafts_done.append(n)
             if all(4 * pair + i in drafts_done for i in range(4)):
@@ -213,8 +189,8 @@ def tile_draft_logit_correction_s9_kernel(tc, x, wd_words, wd_scales, wf, prior,
                     in_=draft_sb[pair][:].rearrange("p n s -> p (n s)"),
                 )
 
-        def turn_e(n):
-            bank = psum.tile([P, 4, P], F32, name="bank")
+        def turn_e(n, b):
+            bank = bank_tile(b, [P, 4, P])
             for j in range(4):
                 nc.tensor.transpose(bank[:, j, :], e_rows[n][:, j, :], ident[:])
             et_banks[n] = bank
@@ -222,8 +198,7 @@ def tile_draft_logit_correction_s9_kernel(tc, x, wd_words, wd_scales, wf, prior,
         def weigh_e(n):
             t, g = divmod(n, 2)
             if g == 0:
-                tile = keep.tile([P, 2, P, 4], BF16, name=f"e_g{t}", align_bytes=64)
-                e_g[t] = tile
+                e_g[t] = keep.tile([P, 2, P, 4], BF16, name=f"stage{4 + t}", align_bytes=64)
             nc.vector.tensor_tensor(
                 out=e_g[t][:, g],
                 in0=et_banks[n][:].rearrange("p j r -> p r j"),
@@ -239,193 +214,196 @@ def tile_draft_logit_correction_s9_kernel(tc, x, wd_words, wd_scales, wf, prior,
             )
             e_q[t], e_s[t] = code, plane
 
-        acc, passes_done = {}, {}
+        acc, cols_done = {}, {}
 
-        def full_mm(block, tiles=range(TILES)):
+        def acc_bank(q, t):
+            return ACC_BANKS[4 * (q % 2) + t]
+
+        def full_mm(block, tiles=range(TILES), lo=0, hi=W):
             panel, q = block
             k = int(panel[1])
-            cols = slice(P * k, P * (k + 1))
+            rows = slice(P * k, P * (k + 1))
             for t in tiles:
-                nth = passes_done.get((q, t), 0)
-                passes_done[q, t] = nth + 1
-                if nth == 0:
-                    bank = psum.tile([P, W], F32, name="bank")
-                    acc[q, t] = bank
+                before = cols_done.get((q, t), 0)
+                cols_done[q, t] = before + hi - lo
+                if before == 0:
+                    acc[q, t] = bank_tile(acc_bank(q, t), [P, W])
                 if panel[0] == "f":
-                    lhs, lhs_s = x_q[t][:, cols].bitcast(E4M3), x_s[t][:, cols]
+                    lhs, lhs_s = x_q[t][:, rows].bitcast(E4M3), x_s[t][:, rows]
                 else:
-                    lhs, lhs_s = e_q[t][:, cols].bitcast(E5M2), e_s[t][:, cols]
+                    lhs, lhs_s = e_q[t][:, rows].bitcast(E5M2), e_s[t][:, rows]
                 nc.tensor.matmul_mx(
-                    out=acc[q, t][:],
+                    out=acc[q, t][:, lo:hi],
                     lhsT=lhs,
                     lhsT_scale=lhs_s,
-                    rhs=codes[block][:].bitcast(E4M3),
-                    rhs_scale=planes[block][:],
-                    start=(nth == 0),
-                    stop=(nth == len(PANELS) - 1),
+                    rhs=codes[block][:, lo:hi].bitcast(E4M3),
+                    rhs_scale=planes[block][:, lo:hi],
+                    start=(before == 0),
+                    stop=(cols_done[q, t] == W * len(PANELS)),
                 )
 
-        def half_mm(block, h, t):
-            panel, q = block
-            k = int(panel[1])
-            cols = slice(h * W // 2, (h + 1) * W // 2)
-            nc.tensor.matmul_mx(
-                out=acc[q, t][:, cols],
-                lhsT=x_q[t][:, P * k : P * (k + 1)].bitcast(E4M3),
-                lhsT_scale=x_s[t][:, P * k : P * (k + 1)],
-                rhs=codes[block][:, cols].bitcast(E4M3),
-                rhs_scale=planes[block][:, cols],
-                start=False,
-                stop=(h == 1),
-            )
-
-        def full_out(q, t, lo=0, hi=W):
-            tile = work.tile([P, hi - lo], F32, name="full_sb", bufs=10)
-            cols = slice(W * q + lo, W * q + hi)
-            nc.vector.tensor_tensor(out=tile[:], in0=acc[q, t][:, lo:hi], in1=bias_bc[:, cols], op=ALU.add)
+        def full_out(q, t):
+            tile = work.tile([P, W], F32, name="full_sb", bufs=10)
+            cols = slice(W * q, W * (q + 1))
+            nc.vector.tensor_tensor(out=tile[:], in0=acc[q, t][:], in1=bias_bc[:, cols], op=ALU.add)
             nc.sync.dma_start(out=full_rows[:, t, cols], in_=tile[:])
 
-        order = [("f0", 0), ("f0", 1), ("f1", 0), ("c0", 0), ("c1", 0), ("f1", 1), ("c0", 1), ("c1", 1)]
-        order = order + [(panel, 2) for panel in PANELS] + [(panel, 3) for panel in ("c0", "c1", "f0", "f1")]
-        turn_x(0)
-        turn_x(1)
-        copy_x(vcopy, 0)
-        quant_x(0)
-        copy_x(vcopy, 1)
-        draft_mm(0)
-        draft_mm(1)
-        quant_x(1)
-        lay(scopy, order[0], 0, 96)
-        lay(vcopy, order[0], 96, 512)
-        turn_x(2)
-        turn_x(3)
-        draft_mm(2)
-        draft_mm(3)
-        exp(0)
-        draft_out(vcopy, 0)
-        exp(1)
-        quant(order[0])
-        draft_out(scopy, 1)
-        copy_x(scopy, 2)
-        lay(vcopy, order[1], 0, 512)
-        copy_x(scopy, 3)
-        turn_e(0)
-        turn_e(1)
-        quant_x(2)
-        quant_x(3)
-        exp(2)
-        exp(3)
-        draft_mm(4)
-        draft_mm(5)
-        turn_e(2)
-        turn_e(3)
-        quant(order[1])
-        lay_gpsimd(order[2], 480)
-        draft_out(scopy, 2)
-        weigh_e(0)
-        weigh_e(1)
-        draft_out(vcopy, 3)
-        weigh_e(2)
-        weigh_e(3)
-        draft_mm(6)
-        draft_mm(7)
-        exp(4)
-        draft_out(scopy, 4)
-        turn_e(4)
-        exp(5)
-        draft_out(scopy, 5)
-        turn_e(5)
-        turn_bias(0)
-        exp(6)
-        exp(7)
-        turn_e(6)
-        turn_bias(1)
-        turn_e(7)
-        quant_e(0)
-        lay(vcopy, order[2], 480, 512)
-        lay(vcopy, order[5], 0, 512)
-        quant_e(1)
-        quant(order[2])
-        lay_gpsimd(order[3], 480)
-        draft_out(scopy, 6)
+
+        load_bias()
+        load_x(0, 1)
+        load_x(1, 1)
+        load_scales()
+        load_wd(0, 1)
+        load_wd(1, 1)
+        load_w("f0", 0, 1)
+        load_x(2, 2)
+        load_prior()
+        load_w("f1", 0, 2)
+        load_w("f0", 1, 1)
+        load_w("c0", 0, 2)
+        load_w("c1", 0, 4)
+        load_w("f0", 2, 2)
+        load_w("f1", 2, 2)
+        load_w("c0", 2, 2)
+
+        turn_bias(0, 4)
+        turn_x(0, 6)
+        turn_x(1, 7)
+        turn_bias(1, 5)
         copy_bias(0)
         copy_bias(1)
-        weigh_e(4)
-        weigh_e(5)
+        copy_x(vcopy, 0, 0)
+        quant_x(0)
+        copy_x(vcopy, 1, 1)
+        quant_x(1)
+        for n in range(3):
+            draft_mm(n, n)
+            exp(n)
+        turn_x(2, 6)
+        draft_mm(3, 3)
+        turn_x(3, 7)
+        turn_e(0, 4)
+        turn_e(1, 5)
+        take_slot(("f0", 0), 1)
+        lay_gpsimd(("f0", 0), 0, 512)
+        draft_out(vcopy, 0)
+        draft_out(vcopy, 1)
+        copy_x(vcopy, 2, 2)
+        draft_out(scopy, 2)
+        exp(3)
+        draft_out(scopy, 3)
+        quant_x(2)
+        copy_x(vcopy, 3, 3)
+        quant(("f0", 0))
+        quant_x(3)
+        draft_mm(4, 2)
+        draft_mm(5, 3)
+        turn_e(2, 0)
+        turn_e(3, 1)
+        draft_mm(6, 6)
+        draft_mm(7, 7)
+        take_slot(("f1", 1), 0)
+        lay(scopy, ("f1", 1), 0, 192)
+        take_slot(("f1", 0), 1)
+        lay_gpsimd(("f1", 0), 0, 400)
+        for n in range(4):
+            weigh_e(n)
+        exp(4)
+        exp(5)
+        draft_out(scopy, 4)
+        draft_out(scopy, 5)
+        turn_e(4, 4)
+        turn_e(5, 5)
+        full_mm(("f0", 0), [0, 1])
+        exp(6)
+        exp(7)
+        turn_e(6, 0)
+        turn_e(7, 1)
+        draft_out(scopy, 6)
+        lay(scopy, ("f1", 1), 192, 512)
+        lay(vcopy, ("f1", 0), 400, 512)
+        quant_e(0)
+        quant_e(1)
+        quant(("f1", 0))
+        take_slot(("f0", 1), 5)
+        lay_gpsimd(("f0", 1), 0, 512)
         draft_out(vcopy, 7)
-        weigh_e(6)
-        weigh_e(7)
-        full_mm(order[0])
-        full_mm(order[2])
-        full_mm(order[1])
-        lay(scopy, order[6], 0, 512)
+        for n in range(4, 8):
+            weigh_e(n)
+        full_mm(("f1", 0), [0, 1])
+        full_mm(("f0", 0), [2, 3])
+        full_mm(("f1", 0), [2, 3])
+        take_slot(("c0", 0), 2)
+        lay(scopy, ("c0", 0), 0, 512)
+        quant(("f1", 1))
         quant_e(2)
-        lay(vcopy, order[3], 480, 512)
-        lay(vcopy, order[7], 0, 224)
+        quant(("f0", 1))
         quant_e(3)
-        lay(scopy, order[4], 0, 512)
-        quant(order[3])
-        full_mm(order[3])
-        quant(order[6])
-        lay(scopy, order[7], 224, 512)
-        quant(order[4])
-        full_mm(order[4])
-        full_mm(order[6])
-        quant(order[5])
-        full_mm(order[5])
-        lay(scopy, order[8], 0, 512)
-        quant(order[7])
-        lay_gpsimd(order[11], 352)
-        full_mm(order[7])
-        full_out(0, 0)
-        full_out(0, 1)
-        full_out(0, 2)
-        full_out(0, 3)
-        lay(scopy, order[9], 0, 512)
-        quant(order[8])
-        full_mm(order[8])
-        lay(vcopy, order[10], 0, 512)
-        lay(scopy, order[11], 352, 512)
-        quant(order[9])
-        full_mm(order[9])
-        lay(scopy, order[13], 0, 512)
-        quant(order[11])
-        full_mm(order[11])
-        quant(order[10])
-        lay_gpsimd(order[12], 448)
-        full_mm(order[10])
-        lay(scopy, order[12], 448, 512)
-        full_out(1, 0)
-        full_out(1, 1)
-        full_out(1, 2)
+        full_mm(("f1", 1))
+        full_mm(("f0", 1))
+        take_slot(("c1", 0), 3)
+        lay(scopy, ("c1", 0), 0, 512)
+        quant(("c0", 0))
+        full_mm(("c0", 0))
+        take_slot(("c0", 1), 1)
+        lay(vcopy, ("c0", 1), 0, 512)
+        quant(("c1", 0))
+        quant(("c0", 1))
+        full_mm(("c1", 0))
+        full_mm(("c0", 1))
+        take_slot(("c1", 1), 0)
+        lay(scopy, ("c1", 1), 0, 512)
+        take_slot(("c1", 2), 3)
+        lay_gpsimd(("c1", 2), 0, 400)
+        for t in range(4):
+            full_out(0, t)
+        take_slot(("f0", 2), 2)
+        lay(scopy, ("f0", 2), 0, 512)
+        quant(("c1", 1))
+        lay(vcopy, ("c1", 2), 400, 512)
+        quant(("f0", 2))
+        quant(("c1", 2))
+        full_mm(("c1", 1))
+        full_mm(("f0", 2))
+        full_mm(("c1", 2))
+        take_slot(("f1", 2), 1)
+        lay(scopy, ("f1", 2), 0, 512)
+        take_slot(("c0", 2), 2)
+        lay_gpsimd(("c0", 2), 0, 288)
+        for t in range(3):
+            full_out(1, t)
+        take_slot(("c1", 3), 4)
+        lay(scopy, ("c1", 3), 0, 320)
+        take_slot(("f0", 3), 0)
+        lay(scopy, ("f0", 3), 0, 512)
+        quant(("f1", 2))
+        lay(vcopy, ("c0", 2), 288, 512)
+        lay(vcopy, ("c1", 3), 320, 512)
+        quant(("c0", 2))
+        quant(("c1", 3))
+        quant(("f0", 3))
+        full_mm(("f1", 2))
+        full_mm(("c0", 2))
+        full_mm(("c1", 3), [0, 1, 2])
+        full_mm(("f0", 3), [0, 1, 2])
+        take_slot(("c0", 3), 4)
+        lay_gpsimd(("c0", 3), 0, 400)
         full_out(1, 3)
-        full_out(2, 0)
-        lay(scopy, order[14], 0, 512)
-        quant(order[13])
-        full_mm(order[13])
-        quant(order[12])
-        full_mm(order[12])
-        lay(scopy, order[15], 0, 256)
-        lay(scopy, order[15], 256, 512)
-        full_out(2, 1)
-        quant(order[14])
-        full_out(2, 2)
-        quant_half(order[15], 0)
-        quant_half(order[15], 1)
-        full_mm(order[14], [0])
-        half_mm(order[15], 0, 0)
-        half_mm(order[15], 1, 0)
-        full_mm(order[14], [1])
-        half_mm(order[15], 0, 1)
-        half_mm(order[15], 1, 1)
-        full_mm(order[14], [2])
-        half_mm(order[15], 0, 2)
-        half_mm(order[15], 1, 2)
-        full_mm(order[14], [3])
-        half_mm(order[15], 0, 3)
-        half_mm(order[15], 1, 3)
+        for t in range(3):
+            full_out(2, t)
+        full_mm(("c1", 3), [3])
+        full_mm(("f0", 3), [3])
+        take_slot(("f1", 3), 1)
+        lay(scopy, ("f1", 3), 0, 256)
+        lay(scopy, ("c0", 3), 400, 512)
+        lay(scopy, ("f1", 3), 256, 512)
+        quant(("f1", 3), 0, 256)
+        quant(("c0", 3))
+        quant(("f1", 3), 256, 512)
+        full_mm(("f1", 3), range(4), 0, 256)
+        for t in range(4):
+            full_mm(("c0", 3), [t])
+            full_mm(("f1", 3), [t], 256, 512)
         full_out(2, 3)
-        full_out(3, 0)
-        full_out(3, 1)
-        full_out(3, 2)
-        full_out(3, 3)
+        for t in range(4):
+            full_out(3, t)

@@ -22,7 +22,7 @@ W = 512
 TILES = T // P
 CHUNKS = V // W
 PANELS = ("f0", "f1", "c0", "c1")
-ACC_BANKS = (2, 3, 6, 7, 4, 5, 0, 1)
+ACC_BANKS = (0, 2, 6, 7, 1, 3, 4, 5)
 
 
 def tile_draft_logit_correction_s9_kernel(tc, x, wd_words, wd_scales, wf, prior, c, bias, draft, full):
@@ -254,12 +254,12 @@ def tile_draft_logit_correction_s9_kernel(tc, x, wd_words, wd_scales, wf, prior,
         load_x(1, 1)
         load_scales()
         load_wd(0, 1)
-        load_wd(1, 1)
         load_w("f0", 0, 1)
-        load_x(2, 2)
-        load_prior()
-        load_w("f1", 0, 2)
+        load_wd(1, 1)
         load_w("f0", 1, 1)
+        load_prior()
+        load_x(2, 2)
+        load_w("f1", 0, 2)
         load_w("c0", 0, 2)
         load_w("c1", 0, 4)
         load_w("f0", 2, 2)
@@ -276,134 +276,134 @@ def tile_draft_logit_correction_s9_kernel(tc, x, wd_words, wd_scales, wf, prior,
         quant_x(0)
         copy_x(vcopy, 1, 1)
         quant_x(1)
-        for n in range(3):
+        take_slot(("f0", 0), 2)
+        lay(vcopy, ("f0", 0), 0, 512)
+        quant(("f0", 0))
+        for n in (0, 2, 1, 3):
             draft_mm(n, n)
             exp(n)
-        turn_x(2, 6)
-        draft_mm(3, 3)
-        turn_x(3, 7)
         turn_e(0, 4)
         turn_e(1, 5)
-        take_slot(("f0", 0), 1)
-        lay_gpsimd(("f0", 0), 0, 512)
+        turn_x(2, 6)
+        turn_x(3, 7)
+        take_slot(("f0", 1), 2)
+        lay_gpsimd(("f0", 1), 0, 480)
         draft_out(vcopy, 0)
-        draft_out(vcopy, 1)
-        copy_x(vcopy, 2, 2)
         draft_out(scopy, 2)
-        exp(3)
+        draft_out(scopy, 1)
         draft_out(scopy, 3)
+        lay(scopy, ("f0", 1), 480, 512)
+        weigh_e(0)
+        weigh_e(1)
+        copy_x(vcopy, 2, 0)
+        copy_x(vcopy, 3, 1)
+        full_mm(("f0", 0), [0, 1])
+        turn_e(2, 1)
+        turn_e(3, 3)
         quant_x(2)
-        copy_x(vcopy, 3, 3)
-        quant(("f0", 0))
         quant_x(3)
-        draft_mm(4, 2)
-        draft_mm(5, 3)
-        turn_e(2, 0)
-        turn_e(3, 1)
+        quant_e(0)
+        quant(("f0", 1))
+        draft_mm(4, 4)
+        draft_mm(5, 5)
         draft_mm(6, 6)
         draft_mm(7, 7)
-        take_slot(("f1", 1), 0)
+        take_slot(("f1", 1), 3)
         lay(scopy, ("f1", 1), 0, 192)
-        take_slot(("f1", 0), 1)
-        lay_gpsimd(("f1", 0), 0, 400)
-        for n in range(4):
-            weigh_e(n)
+        take_slot(("f1", 0), 4)
+        lay_gpsimd(("f1", 0), 0, 384)
+        weigh_e(2)
+        weigh_e(3)
         exp(4)
         exp(5)
-        draft_out(scopy, 4)
-        draft_out(scopy, 5)
-        turn_e(4, 4)
-        turn_e(5, 5)
-        full_mm(("f0", 0), [0, 1])
+        draft_out(vcopy, 4)
+        draft_out(vcopy, 5)
+        turn_e(4, 1)
+        turn_e(5, 3)
         exp(6)
         exp(7)
-        turn_e(6, 0)
-        turn_e(7, 1)
+        turn_e(6, 4)
+        turn_e(7, 5)
         draft_out(scopy, 6)
+        draft_out(scopy, 7)
         lay(scopy, ("f1", 1), 192, 512)
-        lay(vcopy, ("f1", 0), 400, 512)
-        quant_e(0)
+        lay(vcopy, ("f1", 0), 384, 512)
         quant_e(1)
         quant(("f1", 0))
-        take_slot(("f0", 1), 5)
-        lay_gpsimd(("f0", 1), 0, 512)
-        draft_out(vcopy, 7)
+        take_slot(("c0", 0), 5)
+        lay_gpsimd(("c0", 0), 0, 384)
         for n in range(4, 8):
             weigh_e(n)
         full_mm(("f1", 0), [0, 1])
         full_mm(("f0", 0), [2, 3])
         full_mm(("f1", 0), [2, 3])
-        take_slot(("c0", 0), 2)
-        lay(scopy, ("c0", 0), 0, 512)
-        quant(("f1", 1))
-        quant_e(2)
-        quant(("f0", 1))
-        quant_e(3)
-        full_mm(("f1", 1))
         full_mm(("f0", 1))
-        take_slot(("c1", 0), 3)
-        lay(scopy, ("c1", 0), 0, 512)
-        quant(("c0", 0))
-        full_mm(("c0", 0))
         take_slot(("c0", 1), 1)
-        lay(vcopy, ("c0", 1), 0, 512)
-        quant(("c1", 0))
+        lay(scopy, ("c0", 1), 0, 512)
+        quant(("f1", 1))
+        lay(vcopy, ("c0", 0), 384, 512)
+        quant_e(2)
+        quant_e(3)
+        quant(("c0", 0))
+        full_mm(("f1", 1))
+        full_mm(("c0", 0))
+        take_slot(("c1", 0), 3)
+        lay(vcopy, ("c1", 0), 0, 512)
         quant(("c0", 1))
+        quant(("c1", 0))
         full_mm(("c1", 0))
         full_mm(("c0", 1))
-        take_slot(("c1", 1), 0)
+        take_slot(("c1", 1), 4)
         lay(scopy, ("c1", 1), 0, 512)
-        take_slot(("c1", 2), 3)
-        lay_gpsimd(("c1", 2), 0, 400)
-        for t in range(4):
-            full_out(0, t)
-        take_slot(("f0", 2), 2)
-        lay(scopy, ("f0", 2), 0, 512)
+        take_slot(("c1", 2), 0)
+        lay(scopy, ("c1", 2), 0, 320)
+        lay(vcopy, ("c1", 2), 320, 512)
         quant(("c1", 1))
-        lay(vcopy, ("c1", 2), 400, 512)
-        quant(("f0", 2))
         quant(("c1", 2))
         full_mm(("c1", 1))
-        full_mm(("f0", 2))
-        full_mm(("c1", 2))
-        take_slot(("f1", 2), 1)
-        lay(scopy, ("f1", 2), 0, 512)
-        take_slot(("c0", 2), 2)
-        lay_gpsimd(("c0", 2), 0, 288)
-        for t in range(3):
-            full_out(1, t)
-        take_slot(("c1", 3), 4)
-        lay(scopy, ("c1", 3), 0, 320)
-        take_slot(("f0", 3), 0)
-        lay(scopy, ("f0", 3), 0, 512)
+        take_slot(("f0", 2), 2)
+        lay(scopy, ("f0", 2), 0, 512)
+        take_slot(("f1", 2), 0)
+        lay_gpsimd(("f1", 2), 0, 320)
+        for t in range(4):
+            full_out(0, t)
+        take_slot(("c1", 3), 1)
+        lay(scopy, ("c1", 3), 0, 512)
+        lay(vcopy, ("f1", 2), 320, 512)
+        quant(("f0", 2))
         quant(("f1", 2))
-        lay(vcopy, ("c0", 2), 288, 512)
-        lay(vcopy, ("c1", 3), 320, 512)
-        quant(("c0", 2))
-        quant(("c1", 3))
-        quant(("f0", 3))
+        full_mm(("c1", 2))
+        full_mm(("f0", 2))
         full_mm(("f1", 2))
+        take_slot(("c0", 2), 2)
+        lay_gpsimd(("c0", 2), 0, 384)
+        lay(scopy, ("c0", 2), 384, 512)
+        for t in range(4):
+            full_out(1, t)
+        take_slot(("f0", 3), 3)
+        lay(scopy, ("f0", 3), 0, 512)
+        quant(("c1", 3))
+        quant(("c0", 2))
+        quant(("f0", 3))
+        full_mm(("c1", 3), [0, 1])
         full_mm(("c0", 2))
-        full_mm(("c1", 3), [0, 1, 2])
-        full_mm(("f0", 3), [0, 1, 2])
-        take_slot(("c0", 3), 4)
-        lay_gpsimd(("c0", 3), 0, 400)
-        full_out(1, 3)
+        full_mm(("c1", 3), [2, 3])
+        full_mm(("f0", 3))
+        take_slot(("c0", 3), 3)
+        lay_gpsimd(("c0", 3), 0, 224)
+        take_slot(("f1", 3), 4)
+        lay(scopy, ("f1", 3), 0, 256)
+        lay(scopy, ("c0", 3), 224, 512)
         for t in range(3):
             full_out(2, t)
-        full_mm(("c1", 3), [3])
-        full_mm(("f0", 3), [3])
-        take_slot(("f1", 3), 1)
-        lay(scopy, ("f1", 3), 0, 256)
-        lay(scopy, ("c0", 3), 400, 512)
         lay(scopy, ("f1", 3), 256, 512)
         quant(("f1", 3), 0, 256)
         quant(("c0", 3))
         quant(("f1", 3), 256, 512)
+        full_out(2, 3)
         full_mm(("f1", 3), range(4), 0, 256)
         for t in range(4):
             full_mm(("c0", 3), [t])
             full_mm(("f1", 3), [t], 256, 512)
-        full_out(2, 3)
         for t in range(4):
             full_out(3, t)

@@ -356,8 +356,7 @@ def tile_draft_logit_correction_s9_kernel(tc, x, wd_words, wd_scales, wf, prior,
         take_slot(("c1", 1), 4)
         lay(scopy, ("c1", 1), 0, 512)
         take_slot(("c1", 2), 0)
-        lay(scopy, ("c1", 2), 0, 320)
-        lay(vcopy, ("c1", 2), 320, 512)
+        lay(scopy, ("c1", 2), 0, 512)
         quant(("c1", 1))
         quant(("c1", 2))
         full_mm(("c1", 1))
@@ -365,11 +364,11 @@ def tile_draft_logit_correction_s9_kernel(tc, x, wd_words, wd_scales, wf, prior,
         lay(scopy, ("f0", 2), 0, 512)
         take_slot(("f1", 2), 0)
         lay_gpsimd(("f1", 2), 0, 320)
+        lay(scopy, ("f1", 2), 320, 512)
         for t in range(4):
             full_out(0, t)
         take_slot(("c1", 3), 1)
         lay(scopy, ("c1", 3), 0, 512)
-        lay(vcopy, ("f1", 2), 320, 512)
         quant(("f0", 2))
         quant(("f1", 2))
         full_mm(("c1", 2))

@@ -259,7 +259,8 @@ def tile_draft_logit_correction_s9_kernel(tc, x, wd_words, wd_scales, wf, prior,
         load_w("f0", 1, 1)
         load_prior()
         load_x(2, 2)
-        load_w("f1", 0, 2)
+        load_w("f1", 1, 1)
+        load_w("f1", 0, 1)
         load_w("c0", 0, 2)
         load_w("c1", 0, 4)
         load_w("f0", 2, 2)
@@ -271,13 +272,14 @@ def tile_draft_logit_correction_s9_kernel(tc, x, wd_words, wd_scales, wf, prior,
         turn_x(1, 7)
         turn_bias(1, 5)
         copy_bias(0)
-        copy_bias(1)
         copy_x(vcopy, 0, 0)
         quant_x(0)
-        copy_x(vcopy, 1, 1)
+        copy_x(scopy, 1, 1)
+        copy_bias(1)
         quant_x(1)
         take_slot(("f0", 0), 2)
-        lay(vcopy, ("f0", 0), 0, 512)
+        lay(scopy, ("f0", 0), 352, 512)
+        lay(vcopy, ("f0", 0), 0, 352)
         quant(("f0", 0))
         for n in (0, 2, 1, 3):
             draft_mm(n, n)
@@ -287,12 +289,11 @@ def tile_draft_logit_correction_s9_kernel(tc, x, wd_words, wd_scales, wf, prior,
         turn_x(2, 6)
         turn_x(3, 7)
         take_slot(("f0", 1), 2)
-        lay_gpsimd(("f0", 1), 0, 480)
+        lay_gpsimd(("f0", 1), 0, 512)
         draft_out(vcopy, 0)
-        draft_out(scopy, 2)
+        draft_out(vcopy, 2)
         draft_out(scopy, 1)
         draft_out(scopy, 3)
-        lay(scopy, ("f0", 1), 480, 512)
         weigh_e(0)
         weigh_e(1)
         copy_x(vcopy, 2, 0)
@@ -309,9 +310,10 @@ def tile_draft_logit_correction_s9_kernel(tc, x, wd_words, wd_scales, wf, prior,
         draft_mm(6, 6)
         draft_mm(7, 7)
         take_slot(("f1", 1), 3)
-        lay(scopy, ("f1", 1), 0, 192)
+        lay(scopy, ("f1", 1), 0, 512)
         take_slot(("f1", 0), 4)
-        lay_gpsimd(("f1", 0), 0, 384)
+        lay_gpsimd(("f1", 0), 0, 416)
+        lay(scopy, ("f1", 0), 416, 512)
         weigh_e(2)
         weigh_e(3)
         exp(4)
@@ -326,12 +328,11 @@ def tile_draft_logit_correction_s9_kernel(tc, x, wd_words, wd_scales, wf, prior,
         turn_e(7, 5)
         draft_out(scopy, 6)
         draft_out(scopy, 7)
-        lay(scopy, ("f1", 1), 192, 512)
-        lay(vcopy, ("f1", 0), 384, 512)
         quant_e(1)
         quant(("f1", 0))
         take_slot(("c0", 0), 5)
-        lay_gpsimd(("c0", 0), 0, 384)
+        lay_gpsimd(("c0", 0), 0, 416)
+        lay(scopy, ("c0", 0), 416, 512)
         for n in range(4, 8):
             weigh_e(n)
         full_mm(("f1", 0), [0, 1])
@@ -341,7 +342,6 @@ def tile_draft_logit_correction_s9_kernel(tc, x, wd_words, wd_scales, wf, prior,
         take_slot(("c0", 1), 1)
         lay(scopy, ("c0", 1), 0, 512)
         quant(("f1", 1))
-        lay(vcopy, ("c0", 0), 384, 512)
         quant_e(2)
         quant_e(3)
         quant(("c0", 0))
@@ -363,8 +363,8 @@ def tile_draft_logit_correction_s9_kernel(tc, x, wd_words, wd_scales, wf, prior,
         take_slot(("f0", 2), 2)
         lay(scopy, ("f0", 2), 0, 512)
         take_slot(("f1", 2), 0)
-        lay_gpsimd(("f1", 2), 0, 320)
-        lay(scopy, ("f1", 2), 320, 512)
+        lay_gpsimd(("f1", 2), 0, 352)
+        lay(scopy, ("f1", 2), 352, 512)
         for t in range(4):
             full_out(0, t)
         take_slot(("c1", 3), 1)
@@ -375,8 +375,8 @@ def tile_draft_logit_correction_s9_kernel(tc, x, wd_words, wd_scales, wf, prior,
         full_mm(("f0", 2))
         full_mm(("f1", 2))
         take_slot(("c0", 2), 2)
-        lay_gpsimd(("c0", 2), 0, 384)
-        lay(scopy, ("c0", 2), 384, 512)
+        lay_gpsimd(("c0", 2), 0, 416)
+        lay(scopy, ("c0", 2), 416, 512)
         for t in range(4):
             full_out(1, t)
         take_slot(("f0", 3), 3)
@@ -389,10 +389,10 @@ def tile_draft_logit_correction_s9_kernel(tc, x, wd_words, wd_scales, wf, prior,
         full_mm(("c1", 3), [2, 3])
         full_mm(("f0", 3))
         take_slot(("c0", 3), 3)
-        lay_gpsimd(("c0", 3), 0, 224)
+        lay_gpsimd(("c0", 3), 0, 256)
         take_slot(("f1", 3), 4)
         lay(scopy, ("f1", 3), 0, 256)
-        lay(scopy, ("c0", 3), 224, 512)
+        lay(scopy, ("c0", 3), 256, 512)
         for t in range(3):
             full_out(2, t)
         lay(scopy, ("f1", 3), 256, 512)

@@ -243,7 +243,7 @@ def tile_draft_logit_correction_s9_kernel(tc, x, wd_words, wd_scales, wf, prior,
                 )
 
         def full_out(q, t):
-            tile = work.tile([P, W], F32, name="full_sb", bufs=10)
+            tile = keep.tile([P, W], F32, name=f"full_sb{q}_{t}")
             cols = slice(W * q, W * (q + 1))
             nc.vector.tensor_tensor(out=tile[:], in0=acc[q, t][:], in1=bias_bc[:, cols], op=ALU.add)
             nc.sync.dma_start(out=full_rows[:, t, cols], in_=tile[:])
@@ -342,8 +342,8 @@ def tile_draft_logit_correction_s9_kernel(tc, x, wd_words, wd_scales, wf, prior,
         take_slot(("c0", 1), 1)
         lay(scopy, ("c0", 1), 0, 512)
         quant(("f1", 1))
-        quant_e(2)
         quant_e(3)
+        quant_e(2)
         quant(("c0", 0))
         full_mm(("f1", 1))
         full_mm(("c0", 0))
@@ -377,16 +377,16 @@ def tile_draft_logit_correction_s9_kernel(tc, x, wd_words, wd_scales, wf, prior,
         take_slot(("c0", 2), 2)
         lay_gpsimd(("c0", 2), 0, 416)
         lay(scopy, ("c0", 2), 416, 512)
-        for t in range(4):
+        for t in (3, 2, 1, 0):
             full_out(1, t)
         take_slot(("f0", 3), 3)
         lay(scopy, ("f0", 3), 0, 512)
         quant(("c1", 3))
         quant(("c0", 2))
         quant(("f0", 3))
-        full_mm(("c1", 3), [0, 1])
+        full_mm(("c1", 3), [3, 2])
         full_mm(("c0", 2))
-        full_mm(("c1", 3), [2, 3])
+        full_mm(("c1", 3), [1, 0])
         full_mm(("f0", 3))
         take_slot(("c0", 3), 3)
         lay_gpsimd(("c0", 3), 0, 256)

@@ -281,43 +281,46 @@ def tile_draft_logit_correction_s9_kernel(tc, x, wd_words, wd_scales, wf, prior,
         lay(scopy, ("f0", 0), 352, 512)
         lay(vcopy, ("f0", 0), 0, 352)
         quant(("f0", 0))
-        for n in (0, 2, 1, 3):
+        for n in (0, 2, 1):
             draft_mm(n, n)
             exp(n)
         turn_e(0, 4)
+        draft_mm(3, 3)
+        draft_out(scopy, 1)
+        exp(3)
         turn_e(1, 5)
         turn_x(2, 6)
-        turn_x(3, 7)
         take_slot(("f0", 1), 2)
-        lay_gpsimd(("f0", 1), 0, 512)
+        lay_gpsimd(("f0", 1), 0, 448)
         draft_out(vcopy, 0)
         draft_out(vcopy, 2)
-        draft_out(scopy, 1)
         draft_out(scopy, 3)
+        lay(scopy, ("f0", 1), 448, 512)
         weigh_e(0)
         weigh_e(1)
         copy_x(vcopy, 2, 0)
-        copy_x(vcopy, 3, 1)
         full_mm(("f0", 0), [0, 1])
+        turn_x(3, 7)
         turn_e(2, 1)
-        turn_e(3, 3)
-        quant_x(2)
-        quant_x(3)
         quant_e(0)
+        quant_x(2)
+        copy_x(vcopy, 3, 1)
         quant(("f0", 1))
+        quant_x(3)
         draft_mm(4, 4)
         draft_mm(5, 5)
+        turn_e(3, 3)
         draft_mm(6, 6)
         draft_mm(7, 7)
         take_slot(("f1", 1), 3)
         lay(scopy, ("f1", 1), 0, 512)
-        take_slot(("f1", 0), 4)
+        take_slot(("f1", 0), 2)
         lay_gpsimd(("f1", 0), 0, 416)
-        lay(scopy, ("f1", 0), 416, 512)
         weigh_e(2)
         weigh_e(3)
         exp(4)
         exp(5)
+        lay(scopy, ("f1", 0), 416, 512)
         draft_out(vcopy, 4)
         draft_out(vcopy, 5)
         turn_e(4, 1)
@@ -360,7 +363,7 @@ def tile_draft_logit_correction_s9_kernel(tc, x, wd_words, wd_scales, wf, prior,
         quant(("c1", 1))
         quant(("c1", 2))
         full_mm(("c1", 1))
-        take_slot(("f0", 2), 2)
+        take_slot(("f0", 2), 5)
         lay(scopy, ("f0", 2), 0, 512)
         take_slot(("f1", 2), 0)
         lay_gpsimd(("f1", 2), 0, 352)
@@ -374,7 +377,7 @@ def tile_draft_logit_correction_s9_kernel(tc, x, wd_words, wd_scales, wf, prior,
         full_mm(("c1", 2))
         full_mm(("f0", 2))
         full_mm(("f1", 2))
-        take_slot(("c0", 2), 2)
+        take_slot(("c0", 2), 5)
         lay_gpsimd(("c0", 2), 0, 416)
         lay(scopy, ("c0", 2), 416, 512)
         for t in (3, 2, 1, 0):

@@ -45,7 +45,7 @@ def tile_draft_logit_correction_s9_kernel(tc, x, wd_words, wd_scales, wf, prior,
         ident = keep.tile([P, P], F32, name="ident")
         make_identity(nc, ident[:])
 
-        x_sb, raw, wd_w = {}, {}, {}
+        x_sb, raw, raw_tiles, wd_w = {}, {}, {}, {}
 
         def load_x(first, count):
             tile = keep.tile([P, count * D], BF16, name=f"x_sb{first}")
@@ -61,6 +61,8 @@ def tile_draft_logit_correction_s9_kernel(tc, x, wd_words, wd_scales, wf, prior,
             nc.sync.dma_start(out=tile[:], in_=rows[:, :, W * first : W * (first + count)])
             for i in range(count):
                 raw[panel, first + i] = tile[:, :, W * i : W * (i + 1)]
+            for i in range(0, count - 1, 2):
+                raw_tiles[panel, first + i] = tile[:, :, W * i : W * (i + 2)]
 
         def load_wd(first, count):
             tile = keep.tile([P, 2, 2 * W * count], U8, name=f"wd_w{first}", align_bytes=64)
@@ -117,6 +119,28 @@ def tile_draft_logit_correction_s9_kernel(tc, x, wd_words, wd_scales, wf, prior,
             )
             x_g[t] = tile
 
+        def turn_x_half(t, g, b):
+            bank = bank_tile(b, [P, 2, P])
+            words = x_sb[t].bitcast(F32)
+            for u in range(2):
+                nc.tensor.transpose(bank[:, u, :], words[:, 256 * g + u : 256 * (g + 1) : 2], ident[:])
+            x_banks[t, g] = bank
+
+        def copy_x_half(copy, t, g, slot):
+            tile = keep.tile([P, P * 4], BF16, name=f"stage{slot}", align_bytes=64)
+            copy(
+                out=tile[:].bitcast(F32).rearrange("p (r u) -> p r u", u=2),
+                in_=x_banks[t, g][:].rearrange("p u r -> p r u"),
+            )
+            x_g[t, g] = tile
+
+        def quant_x_half(t, g):
+            if g == 0:
+                x_q[t] = keep.tile([P, 2 * P], U32, name=f"x_q{t}", align_bytes=64)
+                x_s[t] = keep.tile([P, 2 * P], U8, name=f"x_s{t}", align_bytes=64)
+            cols = slice(P * g, P * (g + 1))
+            nc.vector.quantize_mx(out=x_q[t][:, cols].bitcast(E4M3), scales=x_s[t][:, cols], in_=x_g[t, g][:])
+
         def quant_x(t):
             code = keep.tile([P, 2 * P], U32, name=f"x_q{t}", align_bytes=64)
             plane = keep.tile([P, 2 * P], U8, name=f"x_s{t}", align_bytes=64)
@@ -128,10 +152,27 @@ def tile_draft_logit_correction_s9_kernel(tc, x, wd_words, wd_scales, wf, prior,
         def take_slot(block, slot):
             grouped[block] = keep.tile([P, W, 4], BF16, name=f"stage{slot}", align_bytes=64)
 
+        def take_pair(panel, first, name):
+            tile = keep.tile([P, 2 * W, 4], BF16, name=name, align_bytes=64)
+            grouped[panel, first, 2] = tile
+            raw[panel, first, 2] = raw_tiles[panel, first]
+
+        def quant_pair(panel, first):
+            code = keep.tile([P, 2 * W], U32, name=f"code_{panel}_{first}", align_bytes=64)
+            plane = keep.tile([P, 2 * W], U8, name=f"plane_{panel}_{first}", align_bytes=64)
+            nc.vector.quantize_mx(
+                out=code[:].bitcast(E4M3),
+                scales=plane[:],
+                in_=grouped[panel, first, 2][:].rearrange("p n j -> p (n j)"),
+            )
+            for i in range(2):
+                codes[panel, first + i] = code[:, W * i : W * (i + 1)]
+                planes[panel, first + i] = plane[:, W * i : W * (i + 1)]
+
         def lay_gpsimd(block, lo, hi):
             nc.gpsimd.tensor_scalar(
-                out=grouped[block][:, lo:hi, :],
-                in0=raw[block][:, :, lo:hi].rearrange("p j n -> p n j"),
+                out=grouped[block][:, lo:hi, :].rearrange("p (c i) j -> p c j i", i=4),
+                in0=raw[block][:, :, lo:hi].rearrange("p j (c i) -> p c j i", i=4),
                 scalar1=1.0,
                 scalar2=0.0,
                 op0=ALU.mult,
@@ -145,13 +186,30 @@ def tile_draft_logit_correction_s9_kernel(tc, x, wd_words, wd_scales, wf, prior,
             )
 
         def quant(block, lo=0, hi=W):
-            if lo == 0:
+            if block not in codes:
                 codes[block] = keep.tile([P, W], U32, name=f"code_{block[0]}_{block[1]}", align_bytes=64)
                 planes[block] = keep.tile([P, W], U8, name=f"plane_{block[0]}_{block[1]}", align_bytes=64)
             nc.vector.quantize_mx(
                 out=codes[block][:, lo:hi].bitcast(E4M3),
                 scales=planes[block][:, lo:hi],
                 in_=grouped[block][:, lo:hi, :].rearrange("p n j -> p (n j)"),
+            )
+
+        def lay_apart(copy, block, lo, slot):
+            tile = keep.tile([P, W - lo, 4], BF16, name=f"stage{slot}", align_bytes=64)
+            grouped[block, lo] = tile
+            copy(
+                out=tile[:].rearrange("p (c i) (h e) -> p c h i e", i=4, e=2),
+                in_=raw[block][:, :, lo:].rearrange("p (h e) (c i) -> p c h i e", i=4, e=2),
+            )
+
+        def quant_apart(block, lo):
+            codes[block] = keep.tile([P, W], U32, name=f"code_{block[0]}_{block[1]}", align_bytes=64)
+            planes[block] = keep.tile([P, W], U8, name=f"plane_{block[0]}_{block[1]}", align_bytes=64)
+            nc.vector.quantize_mx(
+                out=codes[block][:, lo:].bitcast(E4M3),
+                scales=planes[block][:, lo:],
+                in_=grouped[block, lo][:].rearrange("p n j -> p (n j)"),
             )
 
         d_banks, e_rows, et_banks, e_g, e_q, e_s, draft_sb = {}, {}, {}, {}, {}, {}, {}
@@ -242,170 +300,199 @@ def tile_draft_logit_correction_s9_kernel(tc, x, wd_words, wd_scales, wf, prior,
                     stop=(cols_done[q, t] == W * len(PANELS)),
                 )
 
-        def full_out(q, t):
-            tile = keep.tile([P, W], F32, name=f"full_sb{q}_{t}")
-            cols = slice(W * q, W * (q + 1))
-            nc.vector.tensor_tensor(out=tile[:], in0=acc[q, t][:], in1=bias_bc[:, cols], op=ALU.add)
-            nc.sync.dma_start(out=full_rows[:, t, cols], in_=tile[:])
+        full_sb, halves_done = {}, {}
 
+        def result_tile(q, t):
+            key = (q // 2, t)
+            if key not in full_sb:
+                full_sb[key] = keep.tile([P, 2, W], F32, name=f"full_sb{key[0]}_{t}")
+            return full_sb[key][:, q % 2, :]
+
+        def store_result(q, t, joined):
+            key = (q // 2, t)
+            halves_done[key] = halves_done.get(key, 0) + 1
+            if not joined:
+                nc.sync.dma_start(out=full_rows[:, t, W * q : W * (q + 1)], in_=full_sb[key][:, q % 2, :])
+            elif halves_done[key] == 2:
+                cols = slice(2 * W * key[0], 2 * W * (key[0] + 1))
+                nc.sync.dma_start(out=full_rows[:, t, cols], in_=full_sb[key][:].rearrange("p h n -> p (h n)"))
+
+        def full_out(q, t, joined=True):
+            tile = result_tile(q, t)
+            nc.vector.tensor_tensor(out=tile, in0=acc[q, t][:], in1=bias_bc[:, W * q : W * (q + 1)], op=ALU.add)
+            store_result(q, t, joined)
+
+        def full_copy(q, t):
+            scopy(out=result_tile(q, t), in_=acc[q, t][:])
+
+        def full_add(q, t, joined=True):
+            tile = result_tile(q, t)
+            nc.gpsimd.tensor_tensor(out=tile, in0=tile, in1=bias_bc[:, W * q : W * (q + 1)], op=ALU.add)
+            store_result(q, t, joined)
 
         load_bias()
         load_x(0, 1)
         load_x(1, 1)
         load_scales()
-        load_wd(0, 1)
+        load_wd(0, 2)
         load_w("f0", 0, 1)
-        load_wd(1, 1)
         load_w("f0", 1, 1)
         load_prior()
         load_x(2, 2)
-        load_w("f1", 1, 1)
-        load_w("f1", 0, 1)
-        load_w("c0", 0, 2)
+        load_w("f1", 0, 2)
+        load_w("c0", 0, 4)
         load_w("c1", 0, 4)
         load_w("f0", 2, 2)
         load_w("f1", 2, 2)
-        load_w("c0", 2, 2)
-
         turn_bias(0, 4)
-        turn_x(0, 6)
+        turn_x_half(0, 0, 6)
+        turn_x_half(0, 1, 3)
         turn_x(1, 7)
         turn_bias(1, 5)
         copy_bias(0)
-        copy_x(vcopy, 0, 0)
-        quant_x(0)
+        copy_x_half(vcopy, 0, 0, 0)
+        copy_x_half(vcopy, 0, 1, 3)
+        quant_x_half(0, 0)
+        quant_x_half(0, 1)
         copy_x(scopy, 1, 1)
         copy_bias(1)
         quant_x(1)
-        take_slot(("f0", 0), 2)
-        lay(scopy, ("f0", 0), 352, 512)
-        lay(vcopy, ("f0", 0), 0, 352)
-        quant(("f0", 0))
-        for n in (0, 2, 1):
+        take_slot(("f0", 0), 3)
+        lay_apart(scopy, ("f0", 0), 384, 2)
+        lay(vcopy, ("f0", 0), 0, 384)
+        quant_apart(("f0", 0), 384)
+        quant(("f0", 0), 0, 384)
+        for n in range(3):
             draft_mm(n, n)
-            exp(n)
+        exp(0)
+        exp(1)
         turn_e(0, 4)
-        draft_mm(3, 3)
-        draft_out(scopy, 1)
-        exp(3)
         turn_e(1, 5)
+        draft_mm(3, 3)
+        exp(2)
+        draft_out(scopy, 2)
+        exp(3)
         turn_x(2, 6)
+        turn_x(3, 7)
         take_slot(("f0", 1), 2)
-        lay_gpsimd(("f0", 1), 0, 448)
+        lay_gpsimd(("f0", 1), 0, 512)
         draft_out(vcopy, 0)
-        draft_out(vcopy, 2)
+        draft_out(vcopy, 1)
         draft_out(scopy, 3)
-        lay(scopy, ("f0", 1), 448, 512)
         weigh_e(0)
         weigh_e(1)
         copy_x(vcopy, 2, 0)
         full_mm(("f0", 0), [0, 1])
-        turn_x(3, 7)
         turn_e(2, 1)
+        turn_e(3, 3)
+        copy_x(scopy, 3, 1)
         quant_e(0)
         quant_x(2)
-        copy_x(vcopy, 3, 1)
         quant(("f0", 1))
         quant_x(3)
         draft_mm(4, 4)
         draft_mm(5, 5)
-        turn_e(3, 3)
         draft_mm(6, 6)
-        draft_mm(7, 7)
         take_slot(("f1", 1), 3)
-        lay(scopy, ("f1", 1), 0, 512)
+        lay(scopy, ("f1", 1), 0, 320)
         take_slot(("f1", 0), 2)
-        lay_gpsimd(("f1", 0), 0, 416)
+        lay_gpsimd(("f1", 0), 0, 432)
         weigh_e(2)
         weigh_e(3)
         exp(4)
         exp(5)
-        lay(scopy, ("f1", 0), 416, 512)
+        lay(scopy, ("f1", 0), 432, 512)
         draft_out(vcopy, 4)
         draft_out(vcopy, 5)
         turn_e(4, 1)
         turn_e(5, 3)
+        draft_mm(7, 7)
         exp(6)
+        lay(scopy, ("f1", 1), 320, 512)
         exp(7)
         turn_e(6, 4)
         turn_e(7, 5)
-        draft_out(scopy, 6)
         draft_out(scopy, 7)
         quant_e(1)
         quant(("f1", 0))
         take_slot(("c0", 0), 5)
-        lay_gpsimd(("c0", 0), 0, 416)
-        lay(scopy, ("c0", 0), 416, 512)
-        for n in range(4, 8):
-            weigh_e(n)
+        lay_gpsimd(("c0", 0), 0, 512)
+        draft_out(vcopy, 6)
+        weigh_e(4)
+        weigh_e(5)
+        weigh_e(6)
+        weigh_e(7)
         full_mm(("f1", 0), [0, 1])
         full_mm(("f0", 0), [2, 3])
         full_mm(("f1", 0), [2, 3])
         full_mm(("f0", 1))
         take_slot(("c0", 1), 1)
         lay(scopy, ("c0", 1), 0, 512)
-        quant(("f1", 1))
-        quant_e(3)
         quant_e(2)
         quant(("c0", 0))
-        full_mm(("f1", 1))
+        quant_e(3)
         full_mm(("c0", 0))
-        take_slot(("c1", 0), 3)
-        lay(vcopy, ("c1", 0), 0, 512)
-        quant(("c0", 1))
+        take_slot(("c0", 2), 4)
+        lay(vcopy, ("c0", 2), 0, 208)
+        lay(scopy, ("c0", 2), 208, 512)
+        take_slot(("c1", 0), 2)
+        lay(vcopy, ("c1", 0), 0, 352)
+        lay(scopy, ("c1", 0), 352, 512)
+        quant(("f1", 1))
+        full_mm(("f1", 1), [0, 1])
         quant(("c1", 0))
         full_mm(("c1", 0))
+        full_mm(("f1", 1), [2, 3])
+        quant(("c0", 1))
         full_mm(("c0", 1))
-        take_slot(("c1", 1), 4)
+        take_slot(("c1", 1), 0)
         lay(scopy, ("c1", 1), 0, 512)
-        take_slot(("c1", 2), 0)
-        lay(scopy, ("c1", 2), 0, 512)
-        quant(("c1", 1))
-        quant(("c1", 2))
-        full_mm(("c1", 1))
+        quant(("c0", 2))
+        take_slot(("c1", 2), 1)
+        lay_gpsimd(("c1", 2), 0, 448)
         take_slot(("f0", 2), 5)
         lay(scopy, ("f0", 2), 0, 512)
-        take_slot(("f1", 2), 0)
-        lay_gpsimd(("f1", 2), 0, 352)
-        lay(scopy, ("f1", 2), 352, 512)
+        lay(scopy, ("c1", 2), 448, 512)
         for t in range(4):
             full_out(0, t)
-        take_slot(("c1", 3), 1)
-        lay(scopy, ("c1", 3), 0, 512)
+        quant(("c1", 1))
+        full_mm(("c0", 2), [0, 1, 2])
+        full_mm(("c1", 1))
+        full_mm(("c0", 2), [3])
+        quant(("c1", 2))
         quant(("f0", 2))
-        quant(("f1", 2))
         full_mm(("c1", 2))
         full_mm(("f0", 2))
-        full_mm(("f1", 2))
-        take_slot(("c0", 2), 5)
-        lay_gpsimd(("c0", 2), 0, 416)
-        lay(scopy, ("c0", 2), 416, 512)
-        for t in (3, 2, 1, 0):
+        take_slot(("f1", 2), 3)
+        lay(scopy, ("f1", 2), 0, 512)
+        take_slot(("c0", 3), 1)
+        lay_gpsimd(("c0", 3), 0, 448)
+        lay(scopy, ("c0", 3), 448, 512)
+        for t in range(4):
             full_out(1, t)
-        take_slot(("f0", 3), 3)
+        take_slot(("f0", 3), 4)
         lay(scopy, ("f0", 3), 0, 512)
-        quant(("c1", 3))
-        quant(("c0", 2))
+        quant(("f1", 2))
+        quant(("c0", 3))
         quant(("f0", 3))
-        full_mm(("c1", 3), [3, 2])
-        full_mm(("c0", 2))
-        full_mm(("c1", 3), [1, 0])
+        full_mm(("f1", 2))
+        full_mm(("c0", 3))
         full_mm(("f0", 3))
-        take_slot(("c0", 3), 3)
-        lay_gpsimd(("c0", 3), 0, 256)
-        take_slot(("f1", 3), 4)
+        take_slot(("c1", 3), 1)
+        lay_gpsimd(("c1", 3), 0, 320)
+        take_slot(("f1", 3), 0)
         lay(scopy, ("f1", 3), 0, 256)
-        lay(scopy, ("c0", 3), 256, 512)
+        lay(scopy, ("c1", 3), 320, 512)
         for t in range(3):
-            full_out(2, t)
+            full_out(2, t, False)
         lay(scopy, ("f1", 3), 256, 512)
         quant(("f1", 3), 0, 256)
-        quant(("c0", 3))
+        quant(("c1", 3))
         quant(("f1", 3), 256, 512)
-        full_out(2, 3)
+        full_out(2, 3, False)
         full_mm(("f1", 3), range(4), 0, 256)
         for t in range(4):
-            full_mm(("c0", 3), [t])
+            full_mm(("c1", 3), [t])
             full_mm(("f1", 3), [t], 256, 512)
         for t in range(4):
-            full_out(3, t)
+            full_out(3, t, False)

@@ -212,7 +212,8 @@ def tile_draft_logit_correction_s9_kernel(tc, x, wd_words, wd_scales, wf, prior,
                 in_=grouped[block, lo][:].rearrange("p n j -> p (n j)"),
             )
 
-        d_banks, e_rows, et_banks, e_g, e_q, e_s, draft_sb = {}, {}, {}, {}, {}, {}, {}
+        d_banks, e_rows, et_banks, e_g, e_q, e_s = {}, {}, {}, {}, {}, {}
+        draft_sb = keep.tile([P, 2 * TILES, W], F32, name="draft_sb")
         drafts_done = []
 
         def draft_mm(n, b):
@@ -236,15 +237,11 @@ def tile_draft_logit_correction_s9_kernel(tc, x, wd_words, wd_scales, wf, prior,
             e_rows[n] = rows
 
         def draft_out(copy, n):
-            pair = n // 4
-            if pair not in draft_sb:
-                draft_sb[pair] = keep.tile([P, 4, W], F32, name=f"draft_sb{pair}")
-            copy(out=draft_sb[pair][:, n % 4, :], in_=d_banks[n][:])
+            copy(out=draft_sb[:, n, :], in_=d_banks[n][:])
             drafts_done.append(n)
-            if all(4 * pair + i in drafts_done for i in range(4)):
+            if len(drafts_done) == 2 * TILES:
                 nc.sync.dma_start(
-                    out=draft_rows[:, 2 * pair : 2 * pair + 2, :].rearrange("p i s -> p (i s)"),
-                    in_=draft_sb[pair][:].rearrange("p n s -> p (n s)"),
+                    out=draft_rows.rearrange("p i s -> p (i s)"), in_=draft_sb[:].rearrange("p n s -> p (n s)")
                 )
 
         def turn_e(n, b):
@@ -340,9 +337,11 @@ def tile_draft_logit_correction_s9_kernel(tc, x, wd_words, wd_scales, wf, prior,
         load_prior()
         load_x(2, 2)
         load_w("f1", 0, 2)
-        load_w("c0", 0, 4)
-        load_w("c1", 0, 4)
+        load_w("c0", 0, 2)
+        load_w("c1", 0, 2)
+        load_w("c0", 2, 2)
         load_w("f0", 2, 2)
+        load_w("c1", 2, 2)
         load_w("f1", 2, 2)
         turn_bias(0, 4)
         turn_x_half(0, 0, 6)
@@ -396,25 +395,25 @@ def tile_draft_logit_correction_s9_kernel(tc, x, wd_words, wd_scales, wf, prior,
         take_slot(("f1", 1), 3)
         lay(scopy, ("f1", 1), 0, 320)
         take_slot(("f1", 0), 2)
-        lay_gpsimd(("f1", 0), 0, 432)
+        lay_gpsimd(("f1", 0), 0, 512)
         weigh_e(2)
         weigh_e(3)
         exp(4)
         exp(5)
-        lay(scopy, ("f1", 0), 432, 512)
         draft_out(vcopy, 4)
         draft_out(vcopy, 5)
         turn_e(4, 1)
-        turn_e(5, 3)
         draft_mm(7, 7)
+        turn_e(5, 3)
         exp(6)
         lay(scopy, ("f1", 1), 320, 512)
         exp(7)
         turn_e(6, 4)
-        turn_e(7, 5)
         draft_out(scopy, 7)
         quant_e(1)
         quant(("f1", 0))
+        full_mm(("f1", 0), [0, 1])
+        turn_e(7, 5)
         take_slot(("c0", 0), 5)
         lay_gpsimd(("c0", 0), 0, 512)
         draft_out(vcopy, 6)
@@ -422,63 +421,59 @@ def tile_draft_logit_correction_s9_kernel(tc, x, wd_words, wd_scales, wf, prior,
         weigh_e(5)
         weigh_e(6)
         weigh_e(7)
-        full_mm(("f1", 0), [0, 1])
         full_mm(("f0", 0), [2, 3])
         full_mm(("f1", 0), [2, 3])
         full_mm(("f0", 1))
-        take_slot(("c0", 1), 1)
-        lay(scopy, ("c0", 1), 0, 512)
+        take_slot(("c1", 0), 1)
+        lay(scopy, ("c1", 0), 0, 512)
         quant_e(2)
         quant(("c0", 0))
         quant_e(3)
         full_mm(("c0", 0))
-        take_slot(("c0", 2), 4)
-        lay(vcopy, ("c0", 2), 0, 208)
-        lay(scopy, ("c0", 2), 208, 512)
-        take_slot(("c1", 0), 2)
-        lay(vcopy, ("c1", 0), 0, 352)
-        lay(scopy, ("c1", 0), 352, 512)
-        quant(("f1", 1))
-        full_mm(("f1", 1), [0, 1])
         quant(("c1", 0))
         full_mm(("c1", 0))
-        full_mm(("f1", 1), [2, 3])
+        take_slot(("c0", 1), 0)
+        lay(scopy, ("c0", 1), 0, 512)
+        take_slot(("c0", 3), 2)
+        lay(vcopy, ("c0", 3), 0, 512)
+        quant(("f1", 1))
+        full_mm(("f1", 1))
         quant(("c0", 1))
         full_mm(("c0", 1))
-        take_slot(("c1", 1), 0)
+        take_slot(("c1", 1), 4)
         lay(scopy, ("c1", 1), 0, 512)
-        quant(("c0", 2))
-        take_slot(("c1", 2), 1)
-        lay_gpsimd(("c1", 2), 0, 448)
+        take_slot(("c0", 2), 3)
+        lay_gpsimd(("c0", 2), 0, 448)
+        lay(scopy, ("c0", 2), 448, 512)
         take_slot(("f0", 2), 5)
         lay(scopy, ("f0", 2), 0, 512)
-        lay(scopy, ("c1", 2), 448, 512)
         for t in range(4):
             full_out(0, t)
         quant(("c1", 1))
-        full_mm(("c0", 2), [0, 1, 2])
         full_mm(("c1", 1))
-        full_mm(("c0", 2), [3])
-        quant(("c1", 2))
+        quant(("c0", 2))
+        full_mm(("c0", 2))
+        quant(("c0", 3))
         quant(("f0", 2))
-        full_mm(("c1", 2))
         full_mm(("f0", 2))
-        take_slot(("f1", 2), 3)
-        lay(scopy, ("f1", 2), 0, 512)
-        take_slot(("c0", 3), 1)
-        lay_gpsimd(("c0", 3), 0, 448)
-        lay(scopy, ("c0", 3), 448, 512)
+        take_slot(("c1", 2), 1)
+        lay(scopy, ("c1", 2), 0, 512)
+        take_slot(("f1", 2), 2)
+        lay_gpsimd(("f1", 2), 0, 448)
+        lay(scopy, ("f1", 2), 448, 512)
         for t in range(4):
             full_out(1, t)
+        full_mm(("c0", 3))
         take_slot(("f0", 3), 4)
         lay(scopy, ("f0", 3), 0, 512)
+        quant(("c1", 2))
         quant(("f1", 2))
-        quant(("c0", 3))
         quant(("f0", 3))
-        full_mm(("f1", 2))
-        full_mm(("c0", 3))
+        for pair in ((0, 1), (2, 3)):
+            full_mm(("c1", 2), pair)
+            full_mm(("f1", 2), pair)
         full_mm(("f0", 3))
-        take_slot(("c1", 3), 1)
+        take_slot(("c1", 3), 2)
         lay_gpsimd(("c1", 3), 0, 320)
         take_slot(("f1", 3), 0)
         lay(scopy, ("f1", 3), 0, 256)

@@ -40,7 +40,7 @@ def tile_draft_logit_correction_s9_kernel(tc, x, wd_words, wd_scales, wf, prior,
 
         bias_col = keep.tile([P, 16], BF16, name="bias_col")
         prior_sb = keep.tile([P, 2, 4], BF16, name="prior_sb")
-        wd_s = keep.tile([P, 2, S], U8, name="wd_s", align_bytes=64)
+        wd_s = keep.tile([P, 2, S], U8, name="wd_s", align_bytes=256)
         nc.vector.memset(wd_s[:].bitcast(I32), 0)
         ident = keep.tile([P, P], F32, name="ident")
         make_identity(nc, ident[:])
@@ -48,7 +48,7 @@ def tile_draft_logit_correction_s9_kernel(tc, x, wd_words, wd_scales, wf, prior,
         x_sb, raw, raw_tiles, wd_w = {}, {}, {}, {}
 
         def load_x(first, count):
-            tile = keep.tile([P, count * D], BF16, name=f"x_sb{first}")
+            tile = keep.tile([P, count * D], BF16, name=f"x_sb{first}", align_bytes=256)
             nc.sync.dma_start(out=tile[:], in_=x_rows[:, first : first + count, :].rearrange("p i d -> p (i d)"))
             for i in range(count):
                 x_sb[first + i] = tile[:, D * i : D * (i + 1)]
@@ -57,7 +57,7 @@ def tile_draft_logit_correction_s9_kernel(tc, x, wd_words, wd_scales, wf, prior,
             src = wf if panel[0] == "f" else c
             g = int(panel[1])
             rows = src[512 * g : 512 * (g + 1), :].rearrange("(p j) n -> p j n", j=4)
-            tile = keep.tile([P, 4, W * count], BF16, name=f"raw_{panel}_{first}")
+            tile = keep.tile([P, 4, W * count], BF16, name=f"raw_{panel}_{first}", align_bytes=256)
             nc.sync.dma_start(out=tile[:], in_=rows[:, :, W * first : W * (first + count)])
             for i in range(count):
                 raw[panel, first + i] = tile[:, :, W * i : W * (i + 1)]
@@ -65,7 +65,7 @@ def tile_draft_logit_correction_s9_kernel(tc, x, wd_words, wd_scales, wf, prior,
                 raw_tiles[panel, first + i] = tile[:, :, W * i : W * (i + 2)]
 
         def load_wd(first, count):
-            tile = keep.tile([P, 2, 2 * W * count], U8, name=f"wd_w{first}", align_bytes=64)
+            tile = keep.tile([P, 2, 2 * W * count], U8, name=f"wd_w{first}", align_bytes=256)
             words = wd_words.bitcast(I32).rearrange("g p n -> p g n")
             nc.sync.dma_start(out=tile[:].bitcast(I32), in_=words[:, :, W // 2 * first : W // 2 * (first + count)])
             for i in range(count):
@@ -213,7 +213,7 @@ def tile_draft_logit_correction_s9_kernel(tc, x, wd_words, wd_scales, wf, prior,
             )
 
         d_banks, e_rows, et_banks, e_g, e_q, e_s = {}, {}, {}, {}, {}, {}
-        draft_sb = keep.tile([P, 2 * TILES, W], F32, name="draft_sb")
+        draft_sb = keep.tile([P, 2 * TILES, W], F32, name="draft_sb", align_bytes=256)
         drafts_done = []
 
         def draft_mm(n, b):
@@ -302,7 +302,7 @@ def tile_draft_logit_correction_s9_kernel(tc, x, wd_words, wd_scales, wf, prior,
         def result_tile(q, t):
             key = (q // 2, t)
             if key not in full_sb:
-                full_sb[key] = keep.tile([P, 2, W], F32, name=f"full_sb{key[0]}_{t}")
+                full_sb[key] = keep.tile([P, 2, W], F32, name=f"full_sb{key[0]}_{t}", align_bytes=256)
             return full_sb[key][:, q % 2, :]
 
         def store_result(q, t, joined):

@@ -337,9 +337,8 @@ def tile_draft_logit_correction_s9_kernel(tc, x, wd_words, wd_scales, wf, prior,
         load_prior()
         load_x(2, 2)
         load_w("f1", 0, 2)
-        load_w("c0", 0, 2)
+        load_w("c0", 0, 4)
         load_w("c1", 0, 2)
-        load_w("c0", 2, 2)
         load_w("f0", 2, 2)
         load_w("c1", 2, 2)
         load_w("f1", 2, 2)
@@ -366,8 +365,8 @@ def tile_draft_logit_correction_s9_kernel(tc, x, wd_words, wd_scales, wf, prior,
         exp(0)
         exp(1)
         turn_e(0, 4)
-        turn_e(1, 5)
         draft_mm(3, 3)
+        turn_e(1, 5)
         exp(2)
         draft_out(scopy, 2)
         exp(3)
@@ -424,43 +423,44 @@ def tile_draft_logit_correction_s9_kernel(tc, x, wd_words, wd_scales, wf, prior,
         full_mm(("f0", 0), [2, 3])
         full_mm(("f1", 0), [2, 3])
         full_mm(("f0", 1))
-        take_slot(("c1", 0), 1)
-        lay(scopy, ("c1", 0), 0, 512)
+        take_slot(("c0", 1), 1)
+        lay(scopy, ("c0", 1), 0, 512)
+
         quant_e(2)
         quant(("c0", 0))
         quant_e(3)
         full_mm(("c0", 0))
-        quant(("c1", 0))
-        full_mm(("c1", 0))
-        take_slot(("c0", 1), 0)
-        lay(scopy, ("c0", 1), 0, 512)
-        take_slot(("c0", 3), 2)
-        lay(vcopy, ("c0", 3), 0, 512)
-        quant(("f1", 1))
-        full_mm(("f1", 1))
         quant(("c0", 1))
         full_mm(("c0", 1))
+        take_slot(("c1", 0), 0)
+        lay(scopy, ("c1", 0), 0, 512)
+        take_slot(("c0", 2), 2)
+        lay(vcopy, ("c0", 2), 0, 512)
+        quant(("c1", 0))
+        full_mm(("c1", 0))
+        quant(("f1", 1))
+        full_mm(("f1", 1))
+        quant(("c0", 2))
         take_slot(("c1", 1), 4)
         lay(scopy, ("c1", 1), 0, 512)
-        take_slot(("c0", 2), 3)
-        lay_gpsimd(("c0", 2), 0, 448)
-        lay(scopy, ("c0", 2), 448, 512)
+        take_slot(("c0", 3), 3)
+        lay_gpsimd(("c0", 3), 0, 432)
+        lay(scopy, ("c0", 3), 432, 512)
         take_slot(("f0", 2), 5)
         lay(scopy, ("f0", 2), 0, 512)
         for t in range(4):
             full_out(0, t)
+        full_mm(("c0", 2))
         quant(("c1", 1))
         full_mm(("c1", 1))
-        quant(("c0", 2))
-        full_mm(("c0", 2))
         quant(("c0", 3))
         quant(("f0", 2))
         full_mm(("f0", 2))
         take_slot(("c1", 2), 1)
         lay(scopy, ("c1", 2), 0, 512)
-        take_slot(("f1", 2), 2)
-        lay_gpsimd(("f1", 2), 0, 448)
-        lay(scopy, ("f1", 2), 448, 512)
+        take_slot(("f1", 2), 3)
+        lay_gpsimd(("f1", 2), 0, 432)
+        lay(scopy, ("f1", 2), 432, 512)
         for t in range(4):
             full_out(1, t)
         full_mm(("c0", 3))
@@ -473,14 +473,14 @@ def tile_draft_logit_correction_s9_kernel(tc, x, wd_words, wd_scales, wf, prior,
             full_mm(("c1", 2), pair)
             full_mm(("f1", 2), pair)
         full_mm(("f0", 3))
-        take_slot(("c1", 3), 2)
-        lay_gpsimd(("c1", 3), 0, 320)
-        take_slot(("f1", 3), 0)
+        take_slot(("f1", 3), 2)
         lay(scopy, ("f1", 3), 0, 256)
-        lay(scopy, ("c1", 3), 320, 512)
+        take_slot(("c1", 3), 4)
+        lay_gpsimd(("c1", 3), 0, 304)
+        lay(scopy, ("c1", 3), 304, 512)
+        lay(scopy, ("f1", 3), 256, 512)
         for t in range(3):
             full_out(2, t, False)
-        lay(scopy, ("f1", 3), 256, 512)
         quant(("f1", 3), 0, 256)
         quant(("c1", 3))
         quant(("f1", 3), 256, 512)

@@ -337,8 +337,9 @@ def tile_draft_logit_correction_s9_kernel(tc, x, wd_words, wd_scales, wf, prior,
         load_prior()
         load_x(2, 2)
         load_w("f1", 0, 2)
-        load_w("c0", 0, 4)
+        load_w("c0", 0, 2)
         load_w("c1", 0, 2)
+        load_w("c0", 2, 2)
         load_w("f0", 2, 2)
         load_w("c1", 2, 2)
         load_w("f1", 2, 2)
@@ -444,8 +445,8 @@ def tile_draft_logit_correction_s9_kernel(tc, x, wd_words, wd_scales, wf, prior,
         take_slot(("c1", 1), 4)
         lay(scopy, ("c1", 1), 0, 512)
         take_slot(("c0", 3), 3)
-        lay_gpsimd(("c0", 3), 0, 432)
-        lay(scopy, ("c0", 3), 432, 512)
+        lay_gpsimd(("c0", 3), 0, 480)
+        lay(scopy, ("c0", 3), 480, 512)
         take_slot(("f0", 2), 5)
         lay(scopy, ("f0", 2), 0, 512)
         for t in range(4):
@@ -459,8 +460,8 @@ def tile_draft_logit_correction_s9_kernel(tc, x, wd_words, wd_scales, wf, prior,
         take_slot(("c1", 2), 1)
         lay(scopy, ("c1", 2), 0, 512)
         take_slot(("f1", 2), 3)
-        lay_gpsimd(("f1", 2), 0, 432)
-        lay(scopy, ("f1", 2), 432, 512)
+        lay_gpsimd(("f1", 2), 0, 480)
+        lay(scopy, ("f1", 2), 480, 512)
         for t in range(4):
             full_out(1, t)
         full_mm(("c0", 3))
@@ -476,8 +477,8 @@ def tile_draft_logit_correction_s9_kernel(tc, x, wd_words, wd_scales, wf, prior,
         take_slot(("f1", 3), 2)
         lay(scopy, ("f1", 3), 0, 256)
         take_slot(("c1", 3), 4)
-        lay_gpsimd(("c1", 3), 0, 304)
-        lay(scopy, ("c1", 3), 304, 512)
+        lay_gpsimd(("c1", 3), 0, 352)
+        lay(scopy, ("c1", 3), 352, 512)
         lay(scopy, ("f1", 3), 256, 512)
         for t in range(3):
             full_out(2, t, False)

@@ -436,7 +436,8 @@ def tile_draft_logit_correction_s9_kernel(tc, x, wd_words, wd_scales, wf, prior,
         take_slot(("c1", 0), 0)
         lay(scopy, ("c1", 0), 0, 512)
         take_slot(("c0", 2), 2)
-        lay(vcopy, ("c0", 2), 0, 512)
+        lay(vcopy, ("c0", 2), 0, 288)
+        lay(scopy, ("c0", 2), 288, 512)
         quant(("c1", 0))
         full_mm(("c1", 0))
         quant(("f1", 1))

@@ -19,6 +19,7 @@ ALU = mybir.AluOpType
 
 P = 128
 W = 512
+SLOT = 4 * W
 TILES = T // P
 CHUNKS = V // W
 PANELS = ("f0", "f1", "c0", "c1")
@@ -45,7 +46,7 @@ def tile_draft_logit_correction_s9_kernel(tc, x, wd_words, wd_scales, wf, prior,
         ident = keep.tile([P, P], F32, name="ident")
         make_identity(nc, ident[:])
 
-        x_sb, raw, raw_tiles, wd_w = {}, {}, {}, {}
+        x_sb, raw, raw_from, wd_w = {}, {}, {}, {}
 
         def load_x(first, count):
             tile = keep.tile([P, count * D], BF16, name=f"x_sb{first}", align_bytes=256)
@@ -61,8 +62,7 @@ def tile_draft_logit_correction_s9_kernel(tc, x, wd_words, wd_scales, wf, prior,
             nc.sync.dma_start(out=tile[:], in_=rows[:, :, W * first : W * (first + count)])
             for i in range(count):
                 raw[panel, first + i] = tile[:, :, W * i : W * (i + 1)]
-            for i in range(0, count - 1, 2):
-                raw_tiles[panel, first + i] = tile[:, :, W * i : W * (i + 2)]
+                raw_from[panel, first + i] = tile[:, :, W * i :]
 
         def load_wd(first, count):
             tile = keep.tile([P, 2, 2 * W * count], U8, name=f"wd_w{first}", align_bytes=256)
@@ -101,6 +101,12 @@ def tile_draft_logit_correction_s9_kernel(tc, x, wd_words, wd_scales, wf, prior,
                 in_=bias_banks[h][:].rearrange("q i p -> q p i"),
             )
 
+        stage = keep.tile([P, 8 * SLOT], BF16, name="stage", align_bytes=64)
+        slot_of = {}
+
+        def staged(slot, values):
+            return stage[:, SLOT * slot : SLOT * slot + values]
+
         x_banks, x_g, x_q, x_s = {}, {}, {}, {}
 
         def turn_x(t, b):
@@ -112,7 +118,7 @@ def tile_draft_logit_correction_s9_kernel(tc, x, wd_words, wd_scales, wf, prior,
             x_banks[t] = bank
 
         def copy_x(copy, t, slot):
-            tile = keep.tile([P, 2 * P * 4], BF16, name=f"stage{slot}", align_bytes=64)
+            tile = staged(slot, 2 * P * 4)
             copy(
                 out=tile[:].bitcast(F32).rearrange("p (g r u) -> p g r u", g=2, u=2),
                 in_=x_banks[t][:].rearrange("p (g u) r -> p g r u", g=2),
@@ -127,7 +133,7 @@ def tile_draft_logit_correction_s9_kernel(tc, x, wd_words, wd_scales, wf, prior,
             x_banks[t, g] = bank
 
         def copy_x_half(copy, t, g, slot):
-            tile = keep.tile([P, P * 4], BF16, name=f"stage{slot}", align_bytes=64)
+            tile = staged(slot, P * 4)
             copy(
                 out=tile[:].bitcast(F32).rearrange("p (r u) -> p r u", u=2),
                 in_=x_banks[t, g][:].rearrange("p u r -> p r u"),
@@ -150,29 +156,20 @@ def tile_draft_logit_correction_s9_kernel(tc, x, wd_words, wd_scales, wf, prior,
         grouped, codes, planes = {}, {}, {}
 
         def take_slot(block, slot):
-            grouped[block] = keep.tile([P, W, 4], BF16, name=f"stage{slot}", align_bytes=64)
+            slot_of[block] = slot
+            grouped[block] = staged(slot, SLOT).rearrange("p (n j) -> p n j", j=4)
 
-        def take_pair(panel, first, name):
-            tile = keep.tile([P, 2 * W, 4], BF16, name=name, align_bytes=64)
-            grouped[panel, first, 2] = tile
-            raw[panel, first, 2] = raw_tiles[panel, first]
-
-        def quant_pair(panel, first):
-            code = keep.tile([P, 2 * W], U32, name=f"code_{panel}_{first}", align_bytes=64)
-            plane = keep.tile([P, 2 * W], U8, name=f"plane_{panel}_{first}", align_bytes=64)
-            nc.vector.quantize_mx(
-                out=code[:].bitcast(E4M3),
-                scales=plane[:],
-                in_=grouped[panel, first, 2][:].rearrange("p n j -> p (n j)"),
-            )
-            for i in range(2):
-                codes[panel, first + i] = code[:, W * i : W * (i + 1)]
-                planes[panel, first + i] = plane[:, W * i : W * (i + 1)]
+        def quant_pair(first, second):
+            code = keep.tile([P, 2 * W], U32, name=f"code_{first[0]}_{first[1]}", align_bytes=64)
+            plane = keep.tile([P, 2 * W], U8, name=f"plane_{first[0]}_{first[1]}", align_bytes=64)
+            nc.vector.quantize_mx(out=code[:].bitcast(E4M3), scales=plane[:], in_=staged(slot_of[first], 2 * SLOT))
+            codes[first], planes[first] = code[:, :W], plane[:, :W]
+            codes[second], planes[second] = code[:, W:], plane[:, W:]
 
         def lay_gpsimd(block, lo, hi):
             nc.gpsimd.tensor_scalar(
-                out=grouped[block][:, lo:hi, :].rearrange("p (c i) j -> p c j i", i=4),
-                in0=raw[block][:, :, lo:hi].rearrange("p j (c i) -> p c j i", i=4),
+                out=staged(slot_of[block], 4 * hi).rearrange("p (c i j) -> p c j i", i=4, j=4),
+                in0=raw_from[block][:, :, lo:hi].rearrange("p j (c i) -> p c j i", i=4),
                 scalar1=1.0,
                 scalar2=0.0,
                 op0=ALU.mult,
@@ -196,7 +193,7 @@ def tile_draft_logit_correction_s9_kernel(tc, x, wd_words, wd_scales, wf, prior,
             )
 
         def lay_apart(copy, block, lo, slot):
-            tile = keep.tile([P, W - lo, 4], BF16, name=f"stage{slot}", align_bytes=64)
+            tile = staged(slot, 4 * (W - lo)).rearrange("p (n j) -> p n j", j=4)
             grouped[block, lo] = tile
             copy(
                 out=tile[:].rearrange("p (c i) (h e) -> p c h i e", i=4, e=2),
@@ -253,7 +250,8 @@ def tile_draft_logit_correction_s9_kernel(tc, x, wd_words, wd_scales, wf, prior,
         def weigh_e(n):
             t, g = divmod(n, 2)
             if g == 0:
-                e_g[t] = keep.tile([P, 2, P, 4], BF16, name=f"stage{4 + t}", align_bytes=64)
+                start = (7 * SLOT, 4 * SLOT, 0, SLOT // 2)[t]
+                e_g[t] = stage[:, start : start + SLOT // 2].rearrange("p (g r j) -> p g r j", g=2, j=4)
             nc.vector.tensor_tensor(
                 out=e_g[t][:, g],
                 in0=et_banks[n][:].rearrange("p j r -> p r j"),
@@ -268,6 +266,13 @@ def tile_draft_logit_correction_s9_kernel(tc, x, wd_words, wd_scales, wf, prior,
                 out=code[:].bitcast(E5M2), scales=plane[:], in_=e_g[t][:].rearrange("p g r j -> p (g r j)")
             )
             e_q[t], e_s[t] = code, plane
+
+        def quant_e_last_two():
+            code = keep.tile([P, 4 * P], U32, name="e_q23", align_bytes=64)
+            plane = keep.tile([P, 4 * P], U8, name="e_s23", align_bytes=64)
+            nc.vector.quantize_mx(out=code[:].bitcast(E5M2), scales=plane[:], in_=staged(0, SLOT))
+            for i in range(2):
+                e_q[2 + i], e_s[2 + i] = code[:, 2 * P * i : 2 * P * (i + 1)], plane[:, 2 * P * i : 2 * P * (i + 1)]
 
         acc, cols_done = {}, {}
 
@@ -414,36 +419,32 @@ def tile_draft_logit_correction_s9_kernel(tc, x, wd_words, wd_scales, wf, prior,
         quant(("f1", 0))
         full_mm(("f1", 0), [0, 1])
         turn_e(7, 5)
-        take_slot(("c0", 0), 5)
-        lay_gpsimd(("c0", 0), 0, 512)
+        take_slot(("c0", 0), 4)
+        lay_gpsimd(("c0", 0), 0, 576)
         draft_out(vcopy, 6)
-        weigh_e(4)
-        weigh_e(5)
-        weigh_e(6)
-        weigh_e(7)
+        for n in range(4, 8):
+            weigh_e(n)
         full_mm(("f0", 0), [2, 3])
         full_mm(("f1", 0), [2, 3])
         full_mm(("f0", 1))
-        take_slot(("c0", 1), 1)
-        lay(scopy, ("c0", 1), 0, 512)
-
-        quant_e(2)
-        quant(("c0", 0))
-        quant_e(3)
+        take_slot(("c0", 1), 5)
+        lay(scopy, ("c0", 1), 64, 512)
+        quant_pair(("c0", 0), ("c0", 1))
+        quant_e_last_two()
         full_mm(("c0", 0))
-        quant(("c0", 1))
-        full_mm(("c0", 1))
-        take_slot(("c1", 0), 0)
+        full_mm(("c0", 1), [0, 1])
+        take_slot(("c1", 0), 1)
         lay(scopy, ("c1", 0), 0, 512)
         take_slot(("c0", 2), 2)
         lay(vcopy, ("c0", 2), 0, 288)
         lay(scopy, ("c0", 2), 288, 512)
         quant(("c1", 0))
         full_mm(("c1", 0))
+        full_mm(("c0", 1), [2, 3])
         quant(("f1", 1))
         full_mm(("f1", 1))
         quant(("c0", 2))
-        take_slot(("c1", 1), 4)
+        take_slot(("c1", 1), 6)
         lay(scopy, ("c1", 1), 0, 512)
         take_slot(("c0", 3), 3)
         lay_gpsimd(("c0", 3), 0, 480)

from contextlib import ExitStack

import concourse.mybir as mybir
from concourse.masks import make_identity

T, D, S, V = 512, 1024, 1024, 2048
FLOPS = 2 * T * D * S + 2 * T * D * V + 2 * T * S * V

F32 = mybir.dt.float32
BF16 = mybir.dt.bfloat16
I32 = mybir.dt.int32
U32 = mybir.dt.uint32
U8 = mybir.dt.uint8
E4M3 = mybir.dt.float8_e4m3fn_x4
E5M2 = mybir.dt.float8_e5m2_x4
E2M1 = mybir.dt.float4_e2m1fn_x4
ACT = mybir.ActivationFunctionType
ALU = mybir.AluOpType

P = 128
W = 512
SLOT = 4 * W
TILES = T // P
CHUNKS = V // W
PANELS = ("f0", "f1", "c0", "c1")
ACC_BANKS = (0, 2, 6, 7, 1, 3, 4, 5)


def tile_draft_logit_correction_s9_kernel(tc, x, wd_words, wd_scales, wf, prior, c, bias, draft, full):
    nc = tc.nc
    with ExitStack() as ctx:
        keep = ctx.enter_context(tc.tile_pool(name="keep", bufs=1))
        work = ctx.enter_context(tc.tile_pool(name="work", bufs=2))
        psum = ctx.enter_context(tc.psum_pool(name="psum", bufs=1))
        ctx.enter_context(tc.manual_schedule())
        vcopy, scopy = nc.vector.tensor_copy, nc.scalar.copy

        x_rows = x.rearrange("(p i) d -> p i d", i=TILES)
        draft_rows = draft.rearrange("(p i) s -> p i s", i=TILES)
        full_rows = full.rearrange("(p i) v -> p i v", i=TILES)

        bias_col = keep.tile([P, 16], BF16, name="bias_col")
        prior_sb = keep.tile([P, 2, 4], BF16, name="prior_sb")
        wd_s = keep.tile([P, 2, S], U8, name="wd_s", align_bytes=256)
        nc.vector.memset(wd_s[:].bitcast(I32), 0)
        ident = keep.tile([P, P], F32, name="ident")
        make_identity(nc, ident[:])

        x_sb, raw, raw_from, wd_w = {}, {}, {}, {}

        def load_x(first, count):
            tile = keep.tile([P, count * D], BF16, name=f"x_sb{first}", align_bytes=256)
            nc.sync.dma_start(out=tile[:], in_=x_rows[:, first : first + count, :].rearrange("p i d -> p (i d)"))
            for i in range(count):
                x_sb[first + i] = tile[:, D * i : D * (i + 1)]

        def load_w(panel, first, count):
            src = wf if panel[0] == "f" else c
            g = int(panel[1])
            rows = src[512 * g : 512 * (g + 1), :].rearrange("(p j) n -> p j n", j=4)
            tile = keep.tile([P, 4, W * count], BF16, name=f"raw_{panel}_{first}", align_bytes=256)
            nc.sync.dma_start(out=tile[:], in_=rows[:, :, W * first : W * (first + count)])
            for i in range(count):
                raw[panel, first + i] = tile[:, :, W * i : W * (i + 1)]
                raw_from[panel, first + i] = tile[:, :, W * i :]

        def load_wd(first, count):
            tile = keep.tile([P, 2, 2 * W * count], U8, name=f"wd_w{first}", align_bytes=256)
            words = wd_words.bitcast(I32).rearrange("g p n -> p g n")
            nc.sync.dma_start(out=tile[:].bitcast(I32), in_=words[:, :, W // 2 * first : W // 2 * (first + count)])
            for i in range(count):
                wd_w[first + i] = tile[:, :, 2 * W * i : 2 * W * (i + 1)]

        def load_scales():
            scale_rows = wd_scales.bitcast(I32).rearrange("g (quad r) n -> r quad g n", r=4)
            for r in range(4):
                nc.sync.dma_start(out=wd_s[r:P:32, :, :].bitcast(I32), in_=scale_rows[r])

        def load_prior():
            nc.sync.dma_start(out=prior_sb[:], in_=prior.rearrange("(g p j) -> p g j", g=2, j=4))

        def load_bias():
            nc.sync.dma_start(out=bias_col[:], in_=bias.rearrange("(p i) -> p i", i=16))

        def bank_tile(b, shape):
            return psum.tile(shape, F32, name=f"bank{b}")

        bias_bc = keep.tile([P, V], BF16, name="bias_bc")
        bias_banks = {}

        def turn_bias(h, b):
            bank = bank_tile(b, [P, 4, P])
            words = bias_col[:].bitcast(F32)
            for i in range(4):
                nc.tensor.transpose(bank[:, i, :], words[:, 4 * h + i : 4 * h + i + 1].to_broadcast([P, P]), ident[:])
            bias_banks[h] = bank

        def copy_bias(h):
            scopy(
                out=bias_bc[:].bitcast(F32).rearrange("q (p h i) -> q h p i", h=2, i=4)[:, h],
                in_=bias_banks[h][:].rearrange("q i p -> q p i"),
            )

        stage = keep.tile([P, 8 * SLOT], BF16, name="stage", align_bytes=64)
        slot_of = {}

        def staged(slot, values):
            return stage[:, SLOT * slot : SLOT * slot + values]

        x_banks, x_g, x_q, x_s = {}, {}, {}, {}

        def turn_x(t, b):
            bank = bank_tile(b, [P, 4, P])
            words = x_sb[t].bitcast(F32)
            for g in range(2):
                for u in range(2):
                    nc.tensor.transpose(bank[:, 2 * g + u, :], words[:, 256 * g + u : 256 * (g + 1) : 2], ident[:])
            x_banks[t] = bank

        def copy_x(copy, t, slot):
            tile = staged(slot, 2 * P * 4)
            copy(
                out=tile[:].bitcast(F32).rearrange("p (g r u) -> p g r u", g=2, u=2),
                in_=x_banks[t][:].rearrange("p (g u) r -> p g r u", g=2),
            )
            x_g[t] = tile

        def turn_x_half(t, g, b):
            bank = bank_tile(b, [P, 2, P])
            words = x_sb[t].bitcast(F32)
            for u in range(2):
                nc.tensor.transpose(bank[:, u, :], words[:, 256 * g + u : 256 * (g + 1) : 2], ident[:])
            x_banks[t, g] = bank

        def copy_x_half(copy, t, g, slot):
            tile = staged(slot, P * 4)
            copy(
                out=tile[:].bitcast(F32).rearrange("p (r u) -> p r u", u=2),
                in_=x_banks[t, g][:].rearrange("p u r -> p r u"),
            )
            x_g[t, g] = tile

        def quant_x_half(t, g):
            if g == 0:
                x_q[t] = keep.tile([P, 2 * P], U32, name=f"x_q{t}", align_bytes=64)
                x_s[t] = keep.tile([P, 2 * P], U8, name=f"x_s{t}", align_bytes=64)
            cols = slice(P * g, P * (g + 1))
            nc.vector.quantize_mx(out=x_q[t][:, cols].bitcast(E4M3), scales=x_s[t][:, cols], in_=x_g[t, g][:])

        def quant_x(t):
            code = keep.tile([P, 2 * P], U32, name=f"x_q{t}", align_bytes=64)
            plane = keep.tile([P, 2 * P], U8, name=f"x_s{t}", align_bytes=64)
            nc.vector.quantize_mx(out=code[:].bitcast(E4M3), scales=plane[:], in_=x_g[t][:])
            x_q[t], x_s[t] = code, plane

        grouped, codes, planes = {}, {}, {}

        def take_slot(block, slot):
            slot_of[block] = slot
            grouped[block] = staged(slot, SLOT).rearrange("p (n j) -> p n j", j=4)

        def quant_pair(first, second):
            code = keep.tile([P, 2 * W], U32, name=f"code_{first[0]}_{first[1]}", align_bytes=64)
            plane = keep.tile([P, 2 * W], U8, name=f"plane_{first[0]}_{first[1]}", align_bytes=64)
            nc.vector.quantize_mx(out=code[:].bitcast(E4M3), scales=plane[:], in_=staged(slot_of[first], 2 * SLOT))
            codes[first], planes[first] = code[:, :W], plane[:, :W]
            codes[second], planes[second] = code[:, W:], plane[:, W:]

        def lay_gpsimd(block, lo, hi):
            nc.gpsimd.tensor_scalar(
                out=staged(slot_of[block], 4 * hi).rearrange("p (c i j) -> p c j i", i=4, j=4),
                in0=raw_from[block][:, :, lo:hi].rearrange("p j (c i) -> p c j i", i=4),
                scalar1=1.0,
                scalar2=0.0,
                op0=ALU.mult,
                op1=ALU.add,
            )

        def lay(copy, block, lo, hi):
            copy(
                out=grouped[block][:, lo:hi, :].rearrange("p (c i) (h e) -> p c h i e", i=4, e=2),
                in_=raw[block][:, :, lo:hi].rearrange("p (h e) (c i) -> p c h i e", i=4, e=2),
            )

        def quant(block, lo=0, hi=W):
            if block not in codes:
                codes[block] = keep.tile([P, W], U32, name=f"code_{block[0]}_{block[1]}", align_bytes=64)
                planes[block] = keep.tile([P, W], U8, name=f"plane_{block[0]}_{block[1]}", align_bytes=64)
            nc.vector.quantize_mx(
                out=codes[block][:, lo:hi].bitcast(E4M3),
                scales=planes[block][:, lo:hi],
                in_=grouped[block][:, lo:hi, :].rearrange("p n j -> p (n j)"),
            )

        def lay_apart(copy, block, lo, slot):
            tile = staged(slot, 4 * (W - lo)).rearrange("p (n j) -> p n j", j=4)
            grouped[block, lo] = tile
            copy(
                out=tile[:].rearrange("p (c i) (h e) -> p c h i e", i=4, e=2),
                in_=raw[block][:, :, lo:].rearrange("p (h e) (c i) -> p c h i e", i=4, e=2),
            )

        def quant_apart(block, lo):
            codes[block] = keep.tile([P, W], U32, name=f"code_{block[0]}_{block[1]}", align_bytes=64)
            planes[block] = keep.tile([P, W], U8, name=f"plane_{block[0]}_{block[1]}", align_bytes=64)
            nc.vector.quantize_mx(
                out=codes[block][:, lo:].bitcast(E4M3),
                scales=planes[block][:, lo:],
                in_=grouped[block, lo][:].rearrange("p n j -> p (n j)"),
            )

        d_banks, e_rows, et_banks, e_g, e_q, e_s = {}, {}, {}, {}, {}, {}
        draft_sb = keep.tile([P, 2 * TILES, W], F32, name="draft_sb", align_bytes=256)
        drafts_done = []

        def draft_mm(n, b):
            t, g = divmod(n, 2)
            bank = bank_tile(b, [P, W])
            for k in range(2):
                nc.tensor.matmul_mx(
                    out=bank[:],
                    lhsT=x_q[t][:, P * k : P * (k + 1)].bitcast(E4M3),
                    lhsT_scale=x_s[t][:, P * k : P * (k + 1)],
                    rhs=wd_w[g][:, k, :].bitcast(E2M1),
                    rhs_scale=wd_s[:, k, W * g : W * (g + 1)],
                    start=(k == 0),
                    stop=(k == 1),
                )
            d_banks[n] = bank

        def exp(n):
            rows = work.tile([P, 4, P], F32, name="e_rows", bufs=4)
            nc.scalar.activation(out=rows[:], in_=d_banks[n][:].rearrange("t (p j) -> t j p", j=4), func=ACT.Exp)
            e_rows[n] = rows

        def draft_out(copy, n):
            copy(out=draft_sb[:, n, :], in_=d_banks[n][:])
            drafts_done.append(n)
            if len(drafts_done) == 2 * TILES:
                nc.sync.dma_start(
                    out=draft_rows.rearrange("p i s -> p (i s)"), in_=draft_sb[:].rearrange("p n s -> p (n s)")
                )

        def turn_e(n, b):
            bank = bank_tile(b, [P, 4, P])
            for j in range(4):
                nc.tensor.transpose(bank[:, j, :], e_rows[n][:, j, :], ident[:])
            et_banks[n] = bank

        def weigh_e(n):
            t, g = divmod(n, 2)
            if g == 0:
                start = (7 * SLOT, 4 * SLOT, 0, SLOT // 2)[t]
                e_g[t] = stage[:, start : start + SLOT // 2].rearrange("p (g r j) -> p g r j", g=2, j=4)
            nc.vector.tensor_tensor(
                out=e_g[t][:, g],
                in0=et_banks[n][:].rearrange("p j r -> p r j"),
                in1=prior_sb[:, g, :].unsqueeze(1).to_broadcast([P, P, 4]),
                op=ALU.mult,
            )

        def quant_e(t):
            code = keep.tile([P, 2 * P], U32, name=f"e_q{t}", align_bytes=64)
            plane = keep.tile([P, 2 * P], U8, name=f"e_s{t}", align_bytes=64)
            nc.vector.quantize_mx(
                out=code[:].bitcast(E5M2), scales=plane[:], in_=e_g[t][:].rearrange("p g r j -> p (g r j)")
            )
            e_q[t], e_s[t] = code, plane

        def quant_e_last_two():
            code = keep.tile([P, 4 * P], U32, name="e_q23", align_bytes=64)
            plane = keep.tile([P, 4 * P], U8, name="e_s23", align_bytes=64)
            nc.vector.quantize_mx(out=code[:].bitcast(E5M2), scales=plane[:], in_=staged(0, SLOT))
            for i in range(2):
                e_q[2 + i], e_s[2 + i] = code[:, 2 * P * i : 2 * P * (i + 1)], plane[:, 2 * P * i : 2 * P * (i + 1)]

        acc, cols_done = {}, {}

        def acc_bank(q, t):
            return ACC_BANKS[4 * (q % 2) + t]

        def full_mm(block, tiles=range(TILES), lo=0, hi=W):
            panel, q = block
            k = int(panel[1])
            rows = slice(P * k, P * (k + 1))
            for t in tiles:
                before = cols_done.get((q, t), 0)
                cols_done[q, t] = before + hi - lo
                if before == 0:
                    acc[q, t] = bank_tile(acc_bank(q, t), [P, W])
                if panel[0] == "f":
                    lhs, lhs_s = x_q[t][:, rows].bitcast(E4M3), x_s[t][:, rows]
                else:
                    lhs, lhs_s = e_q[t][:, rows].bitcast(E5M2), e_s[t][:, rows]
                nc.tensor.matmul_mx(
                    out=acc[q, t][:, lo:hi],
                    lhsT=lhs,
                    lhsT_scale=lhs_s,
                    rhs=codes[block][:, lo:hi].bitcast(E4M3),
                    rhs_scale=planes[block][:, lo:hi],
                    start=(before == 0),
                    stop=(cols_done[q, t] == W * len(PANELS)),
                )

        full_sb, halves_done = {}, {}

        def result_tile(q, t):
            key = (q // 2, t)
            if key not in full_sb:
                full_sb[key] = keep.tile([P, 2, W], F32, name=f"full_sb{key[0]}_{t}", align_bytes=256)
            return full_sb[key][:, q % 2, :]

        def store_result(q, t, joined):
            key = (q // 2, t)
            halves_done[key] = halves_done.get(key, 0) + 1
            if not joined:
                nc.sync.dma_start(out=full_rows[:, t, W * q : W * (q + 1)], in_=full_sb[key][:, q % 2, :])
            elif halves_done[key] == 2:
                cols = slice(2 * W * key[0], 2 * W * (key[0] + 1))
                nc.sync.dma_start(out=full_rows[:, t, cols], in_=full_sb[key][:].rearrange("p h n -> p (h n)"))

        def full_out(q, t, joined=True):
            tile = result_tile(q, t)
            nc.vector.tensor_tensor(out=tile, in0=acc[q, t][:], in1=bias_bc[:, W * q : W * (q + 1)], op=ALU.add)
            store_result(q, t, joined)

        def full_copy(q, t):
            scopy(out=result_tile(q, t), in_=acc[q, t][:])

        def full_add(q, t, joined=True):
            tile = result_tile(q, t)
            nc.gpsimd.tensor_tensor(out=tile, in0=tile, in1=bias_bc[:, W * q : W * (q + 1)], op=ALU.add)
            store_result(q, t, joined)

        load_bias()
        load_x(0, 1)
        load_x(1, 1)
        load_scales()
        load_wd(0, 2)
        load_w("f0", 0, 1)
        load_w("f0", 1, 1)
        load_prior()
        load_x(2, 2)
        load_w("f1", 0, 2)
        load_w("c0", 0, 2)
        load_w("c1", 0, 2)
        load_w("c0", 2, 2)
        load_w("f0", 2, 2)
        load_w("c1", 2, 2)
        load_w("f1", 2, 2)
        turn_bias(0, 4)
        turn_x_half(0, 0, 6)
        turn_x_half(0, 1, 3)
        turn_x(1, 7)
        turn_bias(1, 5)
        copy_bias(0)
        copy_x_half(vcopy, 0, 0, 0)
        copy_x_half(vcopy, 0, 1, 3)
        quant_x_half(0, 0)
        quant_x_half(0, 1)
        copy_x(scopy, 1, 1)
        copy_bias(1)
        quant_x(1)
        take_slot(("f0", 0), 3)
        lay_apart(scopy, ("f0", 0), 384, 2)
        lay(vcopy, ("f0", 0), 0, 384)
        quant_apart(("f0", 0), 384)
        quant(("f0", 0), 0, 384)
        for n in range(3):
            draft_mm(n, n)
        exp(0)
        exp(1)
        turn_e(0, 4)
        draft_mm(3, 3)
        turn_e(1, 5)
        exp(2)
        draft_out(scopy, 2)
        exp(3)
        turn_x(2, 6)
        turn_x(3, 7)
        take_slot(("f0", 1), 2)
        lay_gpsimd(("f0", 1), 0, 512)
        draft_out(vcopy, 0)
        draft_out(vcopy, 1)
        draft_out(scopy, 3)
        weigh_e(0)
        weigh_e(1)
        copy_x(vcopy, 2, 0)
        full_mm(("f0", 0), [0, 1])
        turn_e(2, 1)
        turn_e(3, 3)
        copy_x(scopy, 3, 1)
        quant_e(0)
        quant_x(2)
        quant(("f0", 1))
        quant_x(3)
        draft_mm(4, 4)
        draft_mm(5, 5)
        draft_mm(6, 6)
        take_slot(("f1", 1), 3)
        lay(scopy, ("f1", 1), 0, 320)
        take_slot(("f1", 0), 2)
        lay_gpsimd(("f1", 0), 0, 512)
        weigh_e(2)
        weigh_e(3)
        exp(4)
        exp(5)
        draft_out(vcopy, 4)
        draft_out(vcopy, 5)
        turn_e(4, 1)
        draft_mm(7, 7)
        turn_e(5, 3)
        exp(6)
        lay(scopy, ("f1", 1), 320, 512)
        exp(7)
        turn_e(6, 4)
        draft_out(scopy, 7)
        quant_e(1)
        quant(("f1", 0))
        full_mm(("f1", 0), [0, 1])
        turn_e(7, 5)
        take_slot(("c0", 0), 4)
        lay_gpsimd(("c0", 0), 0, 576)
        draft_out(vcopy, 6)
        for n in range(4, 8):
            weigh_e(n)
        full_mm(("f0", 0), [2, 3])
        full_mm(("f1", 0), [2, 3])
        full_mm(("f0", 1))
        take_slot(("c0", 1), 5)
        lay(scopy, ("c0", 1), 64, 512)
        quant_pair(("c0", 0), ("c0", 1))
        quant_e_last_two()
        full_mm(("c0", 0))
        full_mm(("c0", 1), [0, 1])
        take_slot(("c1", 0), 1)
        lay(scopy, ("c1", 0), 0, 512)
        take_slot(("c0", 2), 2)
        lay(vcopy, ("c0", 2), 0, 288)
        lay(scopy, ("c0", 2), 288, 512)
        quant(("c1", 0))
        full_mm(("c1", 0))
        full_mm(("c0", 1), [2, 3])
        quant(("f1", 1))
        full_mm(("f1", 1))
        quant(("c0", 2))
        take_slot(("c1", 1), 6)
        lay(scopy, ("c1", 1), 0, 512)
        take_slot(("c0", 3), 3)
        lay_gpsimd(("c0", 3), 0, 480)
        lay(scopy, ("c0", 3), 480, 512)
        take_slot(("f0", 2), 5)
        lay(scopy, ("f0", 2), 0, 512)
        for t in range(4):
            full_out(0, t)
        full_mm(("c0", 2))
        quant(("c1", 1))
        full_mm(("c1", 1))
        quant(("c0", 3))
        quant(("f0", 2))
        full_mm(("f0", 2))
        take_slot(("c1", 2), 1)
        lay(scopy, ("c1", 2), 0, 512)
        take_slot(("f1", 2), 3)
        lay_gpsimd(("f1", 2), 0, 480)
        lay(scopy, ("f1", 2), 480, 512)
        for t in range(4):
            full_out(1, t)
        full_mm(("c0", 3))
        take_slot(("f0", 3), 4)
        lay(scopy, ("f0", 3), 0, 512)
        quant(("c1", 2))
        quant(("f1", 2))
        quant(("f0", 3))
        for pair in ((0, 1), (2, 3)):
            full_mm(("c1", 2), pair)
            full_mm(("f1", 2), pair)
        full_mm(("f0", 3))
        take_slot(("f1", 3), 2)
        lay(scopy, ("f1", 3), 0, 256)
        take_slot(("c1", 3), 4)
        lay_gpsimd(("c1", 3), 0, 352)
        lay(scopy, ("c1", 3), 352, 512)
        lay(scopy, ("f1", 3), 256, 512)
        for t in range(3):
            full_out(2, t, False)
        quant(("f1", 3), 0, 256)
        quant(("c1", 3))
        quant(("f1", 3), 256, 512)
        full_out(2, 3, False)
        full_mm(("f1", 3), range(4), 0, 256)
        for t in range(4):
            full_mm(("c1", 3), [t])
            full_mm(("f1", 3), [t], 256, 512)
        for t in range(4):
            full_out(3, t, False)
